import numpy as np
import ml_dtypes


def mxq(x, axis, fmt="e4m3"):
    dtype, down = {"e4m3": (ml_dtypes.float8_e4m3fn, 7), "e5m2": (ml_dtypes.float8_e5m2, 14)}[fmt]
    v = np.moveaxis(np.asarray(x, np.float32).astype(ml_dtypes.bfloat16).astype(np.float64), axis, -1)
    blocks = v.reshape(v.shape[:-1] + (-1, 32))
    amax = np.abs(blocks).max(-1, keepdims=True)
    byte = np.maximum(np.where(amax > 0, np.frexp(amax)[1] - 1 + 127, 0) - down, 1)
    scale = np.exp2(byte - 127.0)
    codes = (blocks / scale).astype(np.float32).astype(dtype).astype(np.float64)
    return np.moveaxis((codes * scale).reshape(v.shape), -1, axis)


WIDE = False


def mx_kscale(k):
    if not WIDE:
        return np.ones(k)
    levels = np.array([10, -10, 5, -5, 0])
    if k % 512:
        return np.exp2(np.random.permutation(np.resize(levels, k // 32))).repeat(32)
    a = np.empty((k // 512, 16))
    for p in range(k // 512):
        a[p, :8] = np.random.permutation(np.resize(levels, 8))
        for g in range(8):
            far = levels[np.abs(levels - a[p, g]) >= 10]
            a[p, g + 8] = far[np.random.randint(len(far))]
    return np.exp2(a.ravel()).repeat(32)


def f64(x):
    return np.asarray(x).astype(np.float64)


def striped(idx):
    return np.tile(idx.reshape(-1, 16).T, (8, 1)).astype(np.uint16)


def unstriped(offs):
    return offs[:16].T.reshape(-1).astype(np.int64)


def pack_weight(w):
    k, n = w.shape
    w = f64(np.asarray(w, np.float32).astype(ml_dtypes.bfloat16)).reshape(k // 32, 32, n)
    amax = np.abs(w).max(1)
    byte = np.clip(np.where(amax > 0, np.frexp(amax)[1] - 1 + 127 - 7, 1), 1, 254)
    scaled = (w * np.exp2(127.0 - byte)[:, None, :]).reshape(k, n).astype(np.float32)
    words = np.ascontiguousarray(scaled.reshape(k // 512, 128, 4, n).transpose(0, 1, 3, 2)).astype(ml_dtypes.float8_e4m3fn).view(np.uint8)
    return words, np.ascontiguousarray(byte.astype(np.uint8).reshape(k // 512, 16, n))


def unpack_weight(words, scales):
    g, p, n, _ = words.shape
    vals = np.ascontiguousarray(words).view(ml_dtypes.float8_e4m3fn).astype(np.float64) * np.repeat(np.exp2(scales.astype(np.float64) - 127.0), 8, axis=1)[..., None]
    return vals.transpose(0, 1, 3, 2).reshape(g * 512, n)


K, T, S, V, N = 1024, 2048, 1024, 512, 256


def setup_inputs():
    n = np.random.standard_normal
    s = mx_kscale(K)[:, None]
    near = np.random.permutation(S)
    packed_xT = pack_weight(n((K, T)) * s)
    return {
        "x_words": packed_xT[0],
        "x_scales": packed_xT[1],
        "w0": (n((K, N)) / np.sqrt(K) / s).astype(np.float32),
        "w1": (n((K, N)) / np.sqrt(K) / s).astype(np.float32),
        "w2": (n((K, N)) / np.sqrt(K) / s).astype(np.float32),
        "offs": striped(np.random.permutation(T)[:S]),
        "cen": striped(np.random.permutation(S)[:V]),
        "pos1": striped(near[:V]),
        "pos2": striped(near[V:]),
    }


def reference(x_words, x_scales, w0, w1, w2, offs, cen, pos1, pos2):
    xq = unpack_weight(x_words, x_scales)[:, unstriped(offs)]
    m0 = np.tanh(mxq(f64(w1), 0, "e4m3").T @ xq)
    c0 = m0[:, unstriped(cen)]
    y = mxq(f64(w0), 0, "e4m3").T @ xq
    m1 = np.tanh(mxq(f64(w2), 0, "e4m3").T @ xq)
    c1 = m1[:, unstriped(cen)]
    return c0 * y[:, unstriped(pos1)] + c1 * y[:, unstriped(pos2)]

@@ -1,0 +1,180 @@
+from contextlib import ExitStack
+
+import concourse.mybir as mybir
+
+K, T, S, V, N = 1024, 2048, 1024, 512, 256
+FLOPS = 3 * 2 * K * N * S
+
+F32 = mybir.dt.float32
+BF16 = mybir.dt.bfloat16
+I32 = mybir.dt.int32
+U32 = mybir.dt.uint32
+U16 = mybir.dt.uint16
+U8 = mybir.dt.uint8
+FP8X4 = mybir.dt.float8_e4m3fn_x4
+ACT = mybir.ActivationFunctionType
+ALU = mybir.AluOpType
+
+P = 128
+PACK = 4
+K_PASS = P * PACK
+PASSES = K // K_PASS
+HALF = 512
+HALVES = S // HALF
+BLOCKS = N // P
+
+
+def tile_picked_zmodd_tanh_p_kernel(tc, x_words, x_scales, w0, w1, w2, offs, cen, pos1, pos2, out):
+    nc = tc.nc
+    with ExitStack() as ctx:
+        lists = ctx.enter_context(tc.tile_pool(name="lists", bufs=1))
+        keep = ctx.enter_context(tc.tile_pool(name="keep", bufs=1))
+        psum = ctx.enter_context(tc.psum_pool(name="psum", bufs=1))
+
+        offs_t = lists.tile([P, S // 16], U16, name="offs_t")
+        cen_t = lists.tile([P, V // 16], U16, name="cen_t")
+        pos_t = [lists.tile([P, V // 16], U16, name="pos_t%d" % d) for d in range(2)]
+
+        weights = {"y": w0, "a": w1, "b": w2}
+        raw = {}
+        rounded = {}
+        w_codes = {}
+        w_scales = {}
+        for name in weights:
+            for o in range(PASSES):
+                raw[name, o] = keep.tile([P, PACK, N], F32, name="raw_%s%d" % (name, o), align_bytes=64)
+                rounded[name, o] = keep.tile([P, N * PACK], BF16, name="rounded_%s%d" % (name, o), align_bytes=64)
+                w_codes[name, o] = keep.tile([P, N], U32, name="w_codes_%s%d" % (name, o), align_bytes=64)
+                w_scales[name, o] = keep.tile([P, N], U8, name="w_scales_%s%d" % (name, o), align_bytes=64)
+        words = [keep.tile([P, T], U32, name="words%d" % o, align_bytes=64) for o in range(PASSES)]
+        planes = keep.tile([P, T], U8, name="planes", align_bytes=64)
+        x_codes = {}
+        for o in range(PASSES):
+            for h in range(HALVES):
+                x_codes[o, h] = keep.tile([P, HALF], U32, name="x_codes%d%d" % (o, h), align_bytes=64)
+        x_planes = keep.tile([P, S], U8, name="x_planes", align_bytes=64)
+        sums = {}
+        for name in weights:
+            for mb in range(BLOCKS):
+                sums[name, mb] = keep.tile([P, S], F32, name="sums_%s%d" % (name, mb), align_bytes=64)
+        sampled = {}
+        gates = {}
+        terms = {}
+        for mb in range(BLOCKS):
+            for d in range(2):
+                sampled[mb, d] = keep.tile([P, V], F32, name="sampled%d%d" % (mb, d), align_bytes=64)
+                gates[mb, d] = keep.tile([P, V], F32, name="gates%d%d" % (mb, d), align_bytes=64)
+                terms[mb, d] = keep.tile([P, V], F32, name="terms%d%d" % (mb, d), align_bytes=64)
+        result = [keep.tile([P, V], F32, name="result%d" % mb, align_bytes=64) for mb in range(BLOCKS)]
+        warm_in = keep.tile([P, 8], F32, name="warm_in")
+        warm_out = keep.tile([P, 8], F32, name="warm_out")
+        banks = {}
+
+        def load_weights(name, o):
+            rows = weights[name][o * K_PASS:(o + 1) * K_PASS, :]
+            nc.sync.dma_start(out=raw[name, o][:], in_=rows.rearrange("(p j) w -> p j w", j=PACK))
+
+        def load_words(o):
+            nc.sync.dma_start(out=words[o][:].bitcast(I32), in_=x_words[o].rearrange("p n t -> p (n t)").bitcast(I32))
+
+        def interleave(copy, name, o):
+            copy(out=rounded[name, o][:].rearrange("p (c i t) -> p c t i", i=4, t=PACK),
+                 in_=raw[name, o][:].rearrange("p t (c i) -> p c t i", i=4))
+
+        def quantize(name, o):
+            nc.vector.quantize_mx(out=w_codes[name, o][:].bitcast(FP8X4), scales=w_scales[name, o][:], in_=rounded[name, o][:])
+
+        def gather_words(o, h):
+            cols = slice(h * HALF // 16, (h + 1) * HALF // 16)
+            nc.vector.tensor_copy(x_codes[o, h][:], words[o][:].indirect(offs_t[:, cols]))
+
+        def multiply(name, o, first_bank):
+            for mb in range(BLOCKS):
+                for h in range(HALVES):
+                    if o == 0:
+                        tag = "bank%d" % (first_bank + mb * HALVES + h)
+                        banks[name, mb, h] = psum.tile([P, HALF], F32, name=tag, tag=tag)
+                    m_cols = slice(mb * P, (mb + 1) * P)
+                    nc.tensor.matmul_mx(
+                        out=banks[name, mb, h][:],
+                        lhsT=w_codes[name, o][:, m_cols].bitcast(FP8X4),
+                        lhsT_scale=w_scales[name, o][:, m_cols],
+                        rhs=x_codes[o, h][:].bitcast(FP8X4),
+                        rhs_scale=x_planes[PACK * o:P, h * HALF:(h + 1) * HALF],
+                        start=(o == 0),
+                        stop=(o == PASSES - 1),
+                    )
+
+        def evacuate(name, mb, scale):
+            for h in range(HALVES):
+                nc.scalar.activation(sums[name, mb][:, h * HALF:(h + 1) * HALF], banks[name, mb, h][:], ACT.Copy, scale=scale)
+
+        def gate(name, mb, d):
+            nc.scalar.activation(gates[mb, d][:], sums[name, mb][:].indirect(cen_t[:]), ACT.Sigmoid, scale=2.0)
+
+        def sample(mb, d):
+            nc.vector.tensor_copy(sampled[mb, d][:], sums["y", mb][:].indirect(pos_t[d][:]))
+
+        def weigh(mb, d):
+            nc.vector.scalar_tensor_tensor(terms[mb, d][:], gates[mb, d][:], 0.5, sampled[mb, d][:], ALU.subtract, ALU.mult)
+
+        def finish(mb):
+            nc.vector.tensor_tensor(result[mb][:], terms[mb, 0][:], terms[mb, 1][:], ALU.add)
+            nc.sync.dma_start(out=out[mb * P:(mb + 1) * P, :], in_=result[mb][:])
+
+        nc.vector.memset(planes[:].bitcast(I32), 0)
+        nc.vector.memset(warm_in[:], 0.0)
+        nc.sync.dma_start(offs_t[:], offs)
+        nc.scalar.activation(warm_out[:], warm_in[:], ACT.Sigmoid)
+        load_weights("y", 0)
+        for q in range(4):
+            nc.sync.dma_start(out=planes[32 * q:32 * q + PASSES * 4, :].bitcast(I32),
+                              in_=x_scales[:, 4 * q:4 * q + 4, :].bitcast(I32))
+        load_words(0)
+        load_words(1)
+        load_weights("y", 1)
+        load_weights("a", 0)
+        load_weights("a", 1)
+        load_weights("b", 0)
+        nc.sync.dma_start(cen_t[:], cen)
+        load_weights("b", 1)
+        nc.sync.dma_start(pos_t[0][:], pos1)
+        nc.sync.dma_start(pos_t[1][:], pos2)
+
+        nc.vector.tensor_copy(x_planes[:], planes[:].indirect(offs_t[:]))
+        interleave(nc.scalar.copy, "y", 0)
+        quantize("y", 0)
+        gather_words(0, 0)
+        gather_words(0, 1)
+        multiply("y", 0, 0)
+        interleave(nc.scalar.copy, "y", 1)
+        gather_words(1, 0)
+        gather_words(1, 1)
+        quantize("y", 1)
+        multiply("y", 1, 0)
+        interleave(nc.scalar.copy, "a", 0)
+        interleave(nc.vector.tensor_copy, "a", 1)
+        quantize("a", 0)
+        quantize("a", 1)
+        multiply("a", 0, 4)
+        multiply("a", 1, 4)
+        evacuate("y", 0, 2.0)
+        evacuate("y", 1, 2.0)
+        interleave(nc.vector.tensor_copy, "b", 0)
+        interleave(nc.vector.tensor_copy, "b", 1)
+        quantize("b", 0)
+        quantize("b", 1)
+        multiply("b", 0, 0)
+        multiply("b", 1, 0)
+        for mb in range(BLOCKS):
+            evacuate("a", mb, 1.0)
+            gate("a", mb, 0)
+            sample(mb, 0)
+            sample(mb, 1)
+        for mb in range(BLOCKS):
+            weigh(mb, 0)
+        for mb in range(BLOCKS):
+            evacuate("b", mb, 1.0)
+            gate("b", mb, 1)
+            weigh(mb, 1)
+            finish(mb)

@@ -35,92 +35,89 @@ def tile_picked_zmodd_tanh_p_kernel(tc, x_words, x_scales, w0, w1, w2, offs, cen
         cen_t = lists.tile([P, V // 16], U16, name="cen_t")
         pos_t = [lists.tile([P, V // 16], U16, name="pos_t%d" % d) for d in range(2)]
 
+        def held(shape, dtype, name, slot=None):
+            return keep.tile(shape, dtype, name=name, tag=slot or name, align_bytes=64)
+
         weights = {"y": w0, "a": w1, "b": w2}
-        raw = {}
-        rounded = {}
-        w_codes = {}
-        w_scales = {}
-        for name in weights:
-            for o in range(PASSES):
-                raw[name, o] = keep.tile([P, PACK, N], F32, name="raw_%s%d" % (name, o), align_bytes=64)
-                rounded[name, o] = keep.tile([P, N * PACK], BF16, name="rounded_%s%d" % (name, o), align_bytes=64)
-                w_codes[name, o] = keep.tile([P, N], U32, name="w_codes_%s%d" % (name, o), align_bytes=64)
-                w_scales[name, o] = keep.tile([P, N], U8, name="w_scales_%s%d" % (name, o), align_bytes=64)
-        words = [keep.tile([P, T], U32, name="words%d" % o, align_bytes=64) for o in range(PASSES)]
-        planes = keep.tile([P, T], U8, name="planes", align_bytes=64)
-        x_codes = {}
-        for o in range(PASSES):
-            for h in range(HALVES):
-                x_codes[o, h] = keep.tile([P, HALF], U32, name="x_codes%d%d" % (o, h), align_bytes=64)
-        x_planes = keep.tile([P, S], U8, name="x_planes", align_bytes=64)
-        sums = {}
-        for name in weights:
-            for mb in range(BLOCKS):
-                sums[name, mb] = keep.tile([P, S], F32, name="sums_%s%d" % (name, mb), align_bytes=64)
-        sampled = {}
-        gates = {}
-        terms = {}
-        for mb in range(BLOCKS):
-            for d in range(2):
-                sampled[mb, d] = keep.tile([P, V], F32, name="sampled%d%d" % (mb, d), align_bytes=64)
-                gates[mb, d] = keep.tile([P, V], F32, name="gates%d%d" % (mb, d), align_bytes=64)
-                terms[mb, d] = keep.tile([P, V], F32, name="terms%d%d" % (mb, d), align_bytes=64)
-        result = [keep.tile([P, V], F32, name="result%d" % mb, align_bytes=64) for mb in range(BLOCKS)]
-        warm_in = keep.tile([P, 8], F32, name="warm_in")
-        warm_out = keep.tile([P, 8], F32, name="warm_out")
-        banks = {}
+        raw, rounded, w_codes, w_scales, x_codes, banks, rows, sampled, terms = {}, {}, {}, {}, {}, {}, {}, {}, {}
+        words = [held([P, T], U32, "words%d" % o) for o in range(PASSES)]
+        planes = held([P, T], U8, "planes")
+        x_planes = held([P, S], U8, "x_planes")
+        warm_in = held([P, 8], F32, "warm_in")
+        warm_out = held([P, 8], F32, "warm_out")
 
         def load_weights(name, o):
-            rows = weights[name][o * K_PASS:(o + 1) * K_PASS, :]
-            nc.sync.dma_start(out=raw[name, o][:], in_=rows.rearrange("(p j) w -> p j w", j=PACK))
+            raw[name, o] = held([P, PACK, N], F32, "raw_%s%d" % (name, o))
+            k_rows = weights[name][o * K_PASS:(o + 1) * K_PASS, :]
+            nc.sync.dma_start(out=raw[name, o][:], in_=k_rows.rearrange("(p j) w -> p j w", j=PACK))
 
         def load_words(o):
             nc.sync.dma_start(out=words[o][:].bitcast(I32), in_=x_words[o].rearrange("p n t -> p (n t)").bitcast(I32))
 
-        def interleave(copy, name, o):
-            copy(out=rounded[name, o][:].rearrange("p (c i t) -> p c t i", i=4, t=PACK),
-                 in_=raw[name, o][:].rearrange("p t (c i) -> p c t i", i=4))
+        def interleave(name, o):
+            rounded[name, o] = held([P, N * PACK], BF16, "rounded_%s%d" % (name, o))
+            nc.scalar.copy(out=rounded[name, o][:].rearrange("p (c i t) -> p c t i", i=4, t=PACK),
+                           in_=raw[name, o][:].rearrange("p t (c i) -> p c t i", i=4))
 
-        def quantize(name, o):
+        def quantize(name, o, slot=None):
+            w_codes[name, o] = held([P, N], U32, "w_codes_%s%d" % (name, o))
+            w_scales[name, o] = held([P, N], U8, "w_scales_%s%d" % (name, o), slot)
             nc.vector.quantize_mx(out=w_codes[name, o][:].bitcast(FP8X4), scales=w_scales[name, o][:], in_=rounded[name, o][:])
 
-        def gather_words(o, h):
-            cols = slice(h * HALF // 16, (h + 1) * HALF // 16)
-            nc.vector.tensor_copy(x_codes[o, h][:], words[o][:].indirect(offs_t[:, cols]))
+        def gather_words(o, first, count):
+            picked = held([P, count * HALF], U32, "x_codes%d%d" % (o, first))
+            cols = slice(first * HALF // 16, (first + count) * HALF // 16)
+            nc.vector.tensor_copy(picked[:], words[o][:].indirect(offs_t[:, cols]))
+            for h in range(count):
+                x_codes[o, first + h] = picked[:, h * HALF:(h + 1) * HALF]
 
-        def multiply(name, o, first_bank):
-            for mb in range(BLOCKS):
-                for h in range(HALVES):
-                    if o == 0:
-                        tag = "bank%d" % (first_bank + mb * HALVES + h)
-                        banks[name, mb, h] = psum.tile([P, HALF], F32, name=tag, tag=tag)
-                    m_cols = slice(mb * P, (mb + 1) * P)
-                    nc.tensor.matmul_mx(
-                        out=banks[name, mb, h][:],
-                        lhsT=w_codes[name, o][:, m_cols].bitcast(FP8X4),
-                        lhsT_scale=w_scales[name, o][:, m_cols],
-                        rhs=x_codes[o, h][:].bitcast(FP8X4),
-                        rhs_scale=x_planes[PACK * o:P, h * HALF:(h + 1) * HALF],
-                        start=(o == 0),
-                        stop=(o == PASSES - 1),
-                    )
+        def multiply(name, o, first_bank, order):
+            for mb, h in order:
+                if o == 0:
+                    tag = "bank%d" % (first_bank + mb * HALVES + h)
+                    banks[name, mb, h] = psum.tile([P, HALF], F32, name=tag, tag=tag)
+                m_cols = slice(mb * P, (mb + 1) * P)
+                nc.tensor.matmul_mx(
+                    out=banks[name, mb, h][:],
+                    lhsT=w_codes[name, o][:, m_cols].bitcast(FP8X4),
+                    lhsT_scale=w_scales[name, o][:, m_cols],
+                    rhs=x_codes[o, h].bitcast(FP8X4),
+                    rhs_scale=x_planes[PACK * o:P, h * HALF:(h + 1) * HALF],
+                    start=(o == 0),
+                    stop=(o == PASSES - 1),
+                )
 
-        def evacuate(name, mb, scale):
+        def evacuate(emit, name, mb, slot=None):
+            rows[name, mb] = held([P, S], F32, "rows_%s%d" % (name, mb), slot)
             for h in range(HALVES):
-                nc.scalar.activation(sums[name, mb][:, h * HALF:(h + 1) * HALF], banks[name, mb, h][:], ACT.Copy, scale=scale)
+                emit(rows[name, mb][:, h * HALF:(h + 1) * HALF], banks[name, mb, h][:])
 
-        def gate(name, mb, d):
-            nc.scalar.activation(gates[mb, d][:], sums[name, mb][:].indirect(cen_t[:]), ACT.Sigmoid, scale=2.0)
+        def tanh(dst, src):
+            nc.scalar.activation(dst, src, ACT.Tanh)
 
-        def sample(mb, d):
-            nc.vector.tensor_copy(sampled[mb, d][:], sums["y", mb][:].indirect(pos_t[d][:]))
+        def sample(mb, d, slot=None):
+            sampled[mb, d] = held([P, V], F32, "sampled%d%d" % (mb, d), slot)
+            nc.vector.tensor_copy(sampled[mb, d][:], rows["y", mb][:].indirect(pos_t[d][:]))
 
-        def weigh(mb, d):
-            nc.vector.scalar_tensor_tensor(terms[mb, d][:], gates[mb, d][:], 0.5, sampled[mb, d][:], ALU.subtract, ALU.mult)
+        def first_term(mb):
+            terms[mb] = held([P, V], F32, "term%d" % mb)
+            nc.vector.tensor_tensor(terms[mb][:], rows["a", mb][:].indirect(cen_t[:]), sampled[mb, 0][:], ALU.mult)
 
-        def finish(mb):
-            nc.vector.tensor_tensor(result[mb][:], terms[mb, 0][:], terms[mb, 1][:], ALU.add)
-            nc.sync.dma_start(out=out[mb * P:(mb + 1) * P, :], in_=result[mb][:])
+        def finish(mb, pieces):
+            width = V // pieces
+            for piece in range(pieces):
+                cols = slice(piece * width, (piece + 1) * width)
+                entries = slice(piece * width // 16, (piece + 1) * width // 16)
+                gate = held([P, width], F32, "gate%d%d" % (mb, piece))
+                nc.scalar.activation(gate[:], rows["b", mb][:].indirect(cen_t[:, entries]), ACT.Sigmoid, scale=2.0)
+                half_term = held([P, width], F32, "half_term%d%d" % (mb, piece))
+                nc.vector.scalar_tensor_tensor(half_term[:], gate[:], 0.5, sampled[mb, 1][:, cols], ALU.subtract, ALU.mult)
+                result = held([P, width], F32, "result%d%d" % (mb, piece))
+                nc.vector.scalar_tensor_tensor(result[:], half_term[:], 2.0, terms[mb][:, cols], ALU.mult, ALU.add)
+                nc.sync.dma_start(out=out[mb * P:(mb + 1) * P, cols], in_=result[:])
+
+        by_block = [(mb, h) for mb in range(BLOCKS) for h in range(HALVES)]
+        by_half = [(mb, h) for h in range(HALVES) for mb in range(BLOCKS)]
 
         nc.vector.memset(planes[:].bitcast(I32), 0)
         nc.vector.memset(warm_in[:], 0.0)
@@ -131,50 +128,47 @@ def tile_picked_zmodd_tanh_p_kernel(tc, x_words, x_scales, w0, w1, w2, offs, cen
             nc.sync.dma_start(out=planes[32 * q:32 * q + PASSES * 4, :].bitcast(I32),
                               in_=x_scales[:, 4 * q:4 * q + 4, :].bitcast(I32))
         load_words(0)
-        load_words(1)
         load_weights("y", 1)
+        load_words(1)
         load_weights("a", 0)
-        load_weights("a", 1)
         load_weights("b", 0)
-        nc.sync.dma_start(cen_t[:], cen)
-        load_weights("b", 1)
+        load_weights("a", 1)
         nc.sync.dma_start(pos_t[0][:], pos1)
+        load_weights("b", 1)
+        nc.sync.dma_start(cen_t[:], cen)
         nc.sync.dma_start(pos_t[1][:], pos2)
 
         nc.vector.tensor_copy(x_planes[:], planes[:].indirect(offs_t[:]))
-        interleave(nc.scalar.copy, "y", 0)
-        quantize("y", 0)
-        gather_words(0, 0)
-        gather_words(0, 1)
-        multiply("y", 0, 0)
-        interleave(nc.scalar.copy, "y", 1)
-        gather_words(1, 0)
-        gather_words(1, 1)
+        interleave("y", 0)
+        quantize("y", 0, "planes")
+        gather_words(0, 0, HALVES)
+        multiply("y", 0, 0, by_half)
+        interleave("y", 1)
         quantize("y", 1)
-        multiply("y", 1, 0)
-        interleave(nc.scalar.copy, "a", 0)
-        interleave(nc.vector.tensor_copy, "a", 1)
+        for h in range(HALVES):
+            gather_words(1, h, 1)
+        multiply("y", 1, 0, by_half)
+        interleave("a", 0)
         quantize("a", 0)
-        quantize("a", 1)
-        multiply("a", 0, 4)
-        multiply("a", 1, 4)
-        evacuate("y", 0, 2.0)
-        evacuate("y", 1, 2.0)
-        interleave(nc.vector.tensor_copy, "b", 0)
-        interleave(nc.vector.tensor_copy, "b", 1)
+        multiply("a", 0, 4, by_block)
+        evacuate(nc.vector.tensor_copy, "y", 0)
+        interleave("b", 0)
         quantize("b", 0)
+        evacuate(nc.scalar.copy, "y", 1, "raw_b0")
+        multiply("b", 0, 0, by_block)
+        sample(0, 0)
+        interleave("a", 1)
+        quantize("a", 1)
+        multiply("a", 1, 4, by_block)
+        sample(1, 0, "rounded_a1")
+        interleave("b", 1)
         quantize("b", 1)
-        multiply("b", 0, 0)
-        multiply("b", 1, 0)
+        multiply("b", 1, 0, by_block)
+        sample(0, 1, "rounded_b1")
+        sample(1, 1)
         for mb in range(BLOCKS):
-            evacuate("a", mb, 1.0)
-            gate("a", mb, 0)
-            sample(mb, 0)
-            sample(mb, 1)
+            evacuate(tanh, "a", mb)
+            first_term(mb)
         for mb in range(BLOCKS):
-            weigh(mb, 0)
-        for mb in range(BLOCKS):
-            evacuate("b", mb, 1.0)
-            gate("b", mb, 1)
-            weigh(mb, 1)
-            finish(mb)
+            evacuate(nc.scalar.copy, "b", mb)
+            finish(mb, 1 + mb)

@@ -54,15 +54,22 @@ def tile_picked_zmodd_tanh_p_kernel(tc, x_words, x_scales, w0, w1, w2, offs, cen
         def load_words(o):
             nc.sync.dma_start(out=words[o][:].bitcast(I32), in_=x_words[o].rearrange("p n t -> p (n t)").bitcast(I32))
 
-        def interleave(name, o):
-            rounded[name, o] = held([P, N * PACK], BF16, "rounded_%s%d" % (name, o))
-            nc.scalar.copy(out=rounded[name, o][:].rearrange("p (c i t) -> p c t i", i=4, t=PACK),
-                           in_=raw[name, o][:].rearrange("p t (c i) -> p c t i", i=4))
+        def interleave(copy, name, o, dst):
+            copy(out=dst.rearrange("p (c i t) -> p c t i", i=2, t=PACK),
+                 in_=raw[name, o][:].rearrange("p t (c i) -> p c t i", i=2))
 
-        def quantize(name, o, slot=None):
-            w_codes[name, o] = held([P, N], U32, "w_codes_%s%d" % (name, o))
-            w_scales[name, o] = held([P, N], U8, "w_scales_%s%d" % (name, o), slot)
-            nc.vector.quantize_mx(out=w_codes[name, o][:].bitcast(FP8X4), scales=w_scales[name, o][:], in_=rounded[name, o][:])
+        def quantize(name, first, count):
+            codes = held([P, count * N], U32, "w_codes_%s%d" % (name, first))
+            scales = held([P, count * N], U8, "w_scales_%s%d" % (name, first))
+            nc.vector.quantize_mx(out=codes[:].bitcast(FP8X4), scales=scales[:], in_=rounded[name, first][:])
+            for j in range(count):
+                w_codes[name, first + j] = codes[:, j * N:(j + 1) * N]
+                w_scales[name, first + j] = scales[:, j * N:(j + 1) * N]
+
+        def prepare(name, o, copy=nc.scalar.copy):
+            rounded[name, o] = held([P, N * PACK], BF16, "rounded_%s%d" % (name, o))
+            interleave(copy, name, o, rounded[name, o][:])
+            quantize(name, o, 1)
 
         def gather_words(o, first, count):
             picked = held([P, count * HALF], U32, "x_codes%d%d" % (o, first))
@@ -87,21 +94,21 @@ def tile_picked_zmodd_tanh_p_kernel(tc, x_words, x_scales, w0, w1, w2, offs, cen
                     stop=(o == PASSES - 1),
                 )
 
-        def evacuate(emit, name, mb, slot=None):
-            rows[name, mb] = held([P, S], F32, "rows_%s%d" % (name, mb), slot)
-            for h in range(HALVES):
+        def evacuate(emits, name, mb):
+            rows[name, mb] = held([P, S], F32, "rows_%s%d" % (name, mb))
+            for h, emit in enumerate(emits):
                 emit(rows[name, mb][:, h * HALF:(h + 1) * HALF], banks[name, mb, h][:])
 
         def tanh(dst, src):
             nc.scalar.activation(dst, src, ACT.Tanh)
 
-        def sample(mb, d, slot=None):
-            sampled[mb, d] = held([P, V], F32, "sampled%d%d" % (mb, d), slot)
-            nc.vector.tensor_copy(sampled[mb, d][:], rows["y", mb][:].indirect(pos_t[d][:]))
+        def sample(mb, d, dst):
+            sampled[mb, d] = dst
+            nc.vector.tensor_copy(dst, rows["y", mb][:].indirect(pos_t[d][:]))
 
         def first_term(mb):
             terms[mb] = held([P, V], F32, "term%d" % mb)
-            nc.vector.tensor_tensor(terms[mb][:], rows["a", mb][:].indirect(cen_t[:]), sampled[mb, 0][:], ALU.mult)
+            nc.vector.tensor_tensor(terms[mb][:], rows["a", mb][:].indirect(cen_t[:]), sampled[mb, 0], ALU.mult)
 
         def finish(mb, pieces):
             width = V // pieces
@@ -122,53 +129,48 @@ def tile_picked_zmodd_tanh_p_kernel(tc, x_words, x_scales, w0, w1, w2, offs, cen
         nc.vector.memset(planes[:].bitcast(I32), 0)
         nc.vector.memset(warm_in[:], 0.0)
         nc.sync.dma_start(offs_t[:], offs)
+        nc.sync.dma_start(cen_t[:], cen)
         nc.scalar.activation(warm_out[:], warm_in[:], ACT.Sigmoid)
-        load_weights("y", 0)
         for q in range(4):
             nc.sync.dma_start(out=planes[32 * q:32 * q + PASSES * 4, :].bitcast(I32),
                               in_=x_scales[:, 4 * q:4 * q + 4, :].bitcast(I32))
         load_words(0)
-        load_weights("y", 1)
+        load_weights("y", 0)
         load_words(1)
+        load_weights("y", 1)
         load_weights("a", 0)
+        nc.sync.dma_start(pos_t[0][:], pos1)
         load_weights("b", 0)
         load_weights("a", 1)
-        nc.sync.dma_start(pos_t[0][:], pos1)
         load_weights("b", 1)
-        nc.sync.dma_start(cen_t[:], cen)
         nc.sync.dma_start(pos_t[1][:], pos2)
 
         nc.vector.tensor_copy(x_planes[:], planes[:].indirect(offs_t[:]))
-        interleave("y", 0)
-        quantize("y", 0, "planes")
         gather_words(0, 0, HALVES)
-        multiply("y", 0, 0, by_half)
-        interleave("y", 1)
-        quantize("y", 1)
+        prepare("y", 0)
+        multiply("y", 0, 0, by_block)
         for h in range(HALVES):
             gather_words(1, h, 1)
-        multiply("y", 1, 0, by_half)
-        interleave("a", 0)
-        quantize("a", 0)
+        prepare("y", 1)
+        multiply("y", 1, 0, by_block)
+        prepare("a", 0)
         multiply("a", 0, 4, by_block)
-        evacuate(nc.vector.tensor_copy, "y", 0)
-        interleave("b", 0)
-        quantize("b", 0)
-        evacuate(nc.scalar.copy, "y", 1, "raw_b0")
+        evacuate([nc.vector.tensor_copy, nc.scalar.copy], "y", 0)
+        evacuate([nc.scalar.copy, nc.scalar.copy], "y", 1)
+        sample(0, 0, held([P, V], F32, "sampled00")[:])
+        prepare("b", 0, nc.vector.tensor_copy)
         multiply("b", 0, 0, by_block)
-        sample(0, 0)
-        interleave("a", 1)
-        quantize("a", 1)
+        prepare("a", 1)
         multiply("a", 1, 4, by_block)
-        sample(1, 0, "rounded_a1")
-        interleave("b", 1)
-        quantize("b", 1)
+        sample(1, 0, held([P, V], F32, "sampled10", "rounded_a1")[:])
+        prepare("b", 1)
         multiply("b", 1, 0, by_block)
-        sample(0, 1, "rounded_b1")
-        sample(1, 1)
+        second_tap = held([P, BLOCKS, V], F32, "second_tap", "rounded_b1")
         for mb in range(BLOCKS):
-            evacuate(tanh, "a", mb)
+            sample(mb, 1, second_tap[:, mb, :])
+        for mb in range(BLOCKS):
+            evacuate([tanh, tanh], "a", mb)
             first_term(mb)
         for mb in range(BLOCKS):
-            evacuate(nc.scalar.copy, "b", mb)
+            evacuate([nc.scalar.copy, nc.scalar.copy], "b", mb)
             finish(mb, 1 + mb)

@@ -39,12 +39,12 @@ def tile_picked_zmodd_tanh_p_kernel(tc, x_words, x_scales, w0, w1, w2, offs, cen
             return keep.tile(shape, dtype, name=name, tag=slot or name, align_bytes=64)
 
         weights = {"y": w0, "a": w1, "b": w2}
-        raw, rounded, w_codes, w_scales, x_codes, banks, rows, sampled, terms = {}, {}, {}, {}, {}, {}, {}, {}, {}
+        raw, rounded, w_codes, w_scales, x_codes, banks, rows, sampled, gates, terms = {}, {}, {}, {}, {}, {}, {}, {}, {}, {}
         words = [held([P, T], U32, "words%d" % o) for o in range(PASSES)]
         planes = held([P, T], U8, "planes")
-        x_planes = held([P, S], U8, "x_planes")
-        warm_in = held([P, 8], F32, "warm_in")
-        warm_out = held([P, 8], F32, "warm_out")
+        x_planes = {}
+        zero = held([P, 1], F32, "zero")
+        centre = held([P, 1], F32, "centre")
 
         def load_weights(name, o):
             raw[name, o] = held([P, PACK, N], F32, "raw_%s%d" % (name, o))
@@ -54,11 +54,20 @@ def tile_picked_zmodd_tanh_p_kernel(tc, x_words, x_scales, w0, w1, w2, offs, cen
         def load_words(o):
             nc.sync.dma_start(out=words[o][:].bitcast(I32), in_=x_words[o].rearrange("p n t -> p (n t)").bitcast(I32))
 
-        def interleave(copy, name, o, dst):
+        def load_scales(queue):
+            for q in range(4):
+                queue.dma_start(out=planes[32 * q:32 * q + PASSES * 4, :].bitcast(I32),
+                                in_=x_scales[:, 4 * q:4 * q + 4, :].bitcast(I32))
+
+        def interleave(copy, name, o, joint=False):
+            first = 0 if joint else o
+            if o == first:
+                rounded[name, first] = held([P, (PASSES if joint else 1) * N * PACK], BF16, "rounded_%s%d" % (name, first))
+            dst = rounded[name, first][:, (o - first) * N * PACK:(o - first + 1) * N * PACK]
             copy(out=dst.rearrange("p (c i t) -> p c t i", i=2, t=PACK),
                  in_=raw[name, o][:].rearrange("p t (c i) -> p c t i", i=2))
 
-        def quantize(name, first, count):
+        def quantize(name, first, count=1):
             codes = held([P, count * N], U32, "w_codes_%s%d" % (name, first))
             scales = held([P, count * N], U8, "w_scales_%s%d" % (name, first))
             nc.vector.quantize_mx(out=codes[:].bitcast(FP8X4), scales=scales[:], in_=rounded[name, first][:])
@@ -66,111 +75,142 @@ def tile_picked_zmodd_tanh_p_kernel(tc, x_words, x_scales, w0, w1, w2, offs, cen
                 w_codes[name, first + j] = codes[:, j * N:(j + 1) * N]
                 w_scales[name, first + j] = scales[:, j * N:(j + 1) * N]
 
-        def prepare(name, o, copy=nc.scalar.copy):
-            rounded[name, o] = held([P, N * PACK], BF16, "rounded_%s%d" % (name, o))
-            interleave(copy, name, o, rounded[name, o][:])
-            quantize(name, o, 1)
+        def gather_scales(first, count, slot=None):
+            picked = held([P, count * HALF], U8, "x_planes%d" % first, slot)
+            cols = slice(first * HALF // 16, (first + count) * HALF // 16)
+            nc.vector.tensor_copy(picked[:], planes[:].indirect(offs_t[:, cols]))
+            for h in range(count):
+                x_planes[first + h] = picked[:, h * HALF:(h + 1) * HALF]
 
-        def gather_words(o, first, count):
-            picked = held([P, count * HALF], U32, "x_codes%d%d" % (o, first))
+        def gather_words(o, first, count, slot=None):
+            picked = held([P, count * HALF], U32, "x_codes%d%d" % (o, first), slot)
             cols = slice(first * HALF // 16, (first + count) * HALF // 16)
             nc.vector.tensor_copy(picked[:], words[o][:].indirect(offs_t[:, cols]))
             for h in range(count):
                 x_codes[o, first + h] = picked[:, h * HALF:(h + 1) * HALF]
 
-        def multiply(name, o, first_bank, order):
-            for mb, h in order:
-                if o == 0:
-                    tag = "bank%d" % (first_bank + mb * HALVES + h)
-                    banks[name, mb, h] = psum.tile([P, HALF], F32, name=tag, tag=tag)
-                m_cols = slice(mb * P, (mb + 1) * P)
-                nc.tensor.matmul_mx(
-                    out=banks[name, mb, h][:],
-                    lhsT=w_codes[name, o][:, m_cols].bitcast(FP8X4),
-                    lhsT_scale=w_scales[name, o][:, m_cols],
-                    rhs=x_codes[o, h].bitcast(FP8X4),
-                    rhs_scale=x_planes[PACK * o:P, h * HALF:(h + 1) * HALF],
-                    start=(o == 0),
-                    stop=(o == PASSES - 1),
-                )
+        def multiply(name, o, first_bank, mb, h):
+            if o == 0:
+                tag = "bank%d" % (first_bank + mb * HALVES + h)
+                banks[name, mb, h] = psum.tile([P, HALF], F32, name=tag, tag=tag)
+            m_cols = slice(mb * P, (mb + 1) * P)
+            nc.tensor.matmul_mx(
+                out=banks[name, mb, h][:],
+                lhsT=w_codes[name, o][:, m_cols].bitcast(FP8X4),
+                lhsT_scale=w_scales[name, o][:, m_cols],
+                rhs=x_codes[o, h].bitcast(FP8X4),
+                rhs_scale=x_planes[h][PACK * o:P, :],
+                start=(o == 0),
+                stop=(o == PASSES - 1),
+            )
 
-        def evacuate(emits, name, mb):
-            rows[name, mb] = held([P, S], F32, "rows_%s%d" % (name, mb))
-            for h, emit in enumerate(emits):
-                emit(rows[name, mb][:, h * HALF:(h + 1) * HALF], banks[name, mb, h][:])
+        def evacuate(emit, name, mb, h):
+            if (name, mb) not in rows:
+                rows[name, mb] = held([P, S], F32, "rows_%s%d" % (name, mb))[:]
+            emit(rows[name, mb][:, h * HALF:(h + 1) * HALF], banks[name, mb, h][:])
+
+        def doubled(dst, src):
+            nc.scalar.activation(dst, src, ACT.Copy, scale=2.0)
+
+        def doubled_v(dst, src):
+            nc.vector.tensor_scalar(dst, src, 2.0, None, ALU.mult)
 
         def tanh(dst, src):
             nc.scalar.activation(dst, src, ACT.Tanh)
 
-        def sample(mb, d, dst):
-            sampled[mb, d] = dst
-            nc.vector.tensor_copy(dst, rows["y", mb][:].indirect(pos_t[d][:]))
+        def sample(mb, d, slot=None):
+            sampled[mb, d] = held([P, V], F32, "sampled%d%d" % (mb, d), slot)
+            nc.vector.tensor_copy(sampled[mb, d][:], rows["y", mb].indirect(pos_t[d][:]))
 
-        def first_term(mb):
-            terms[mb] = held([P, V], F32, "term%d" % mb)
-            nc.vector.tensor_tensor(terms[mb][:], rows["a", mb][:].indirect(cen_t[:]), sampled[mb, 0], ALU.mult)
+        def gate(name, mb, first=0, width=V):
+            gates[name, mb, first] = held([P, width], F32, "gate_%s%d_%d" % (name, mb, first))
+            entries = cen_t[:, first // 16:(first + width) // 16]
+            nc.scalar.activation(gates[name, mb, first][:], rows[name, mb].indirect(entries), ACT.Sigmoid, scale=2.0)
 
-        def finish(mb, pieces):
-            width = V // pieces
-            for piece in range(pieces):
-                cols = slice(piece * width, (piece + 1) * width)
-                entries = slice(piece * width // 16, (piece + 1) * width // 16)
-                gate = held([P, width], F32, "gate%d%d" % (mb, piece))
-                nc.scalar.activation(gate[:], rows["b", mb][:].indirect(cen_t[:, entries]), ACT.Sigmoid, scale=2.0)
-                half_term = held([P, width], F32, "half_term%d%d" % (mb, piece))
-                nc.vector.scalar_tensor_tensor(half_term[:], gate[:], 0.5, sampled[mb, 1][:, cols], ALU.subtract, ALU.mult)
-                result = held([P, width], F32, "result%d%d" % (mb, piece))
-                nc.vector.scalar_tensor_tensor(result[:], half_term[:], 2.0, terms[mb][:, cols], ALU.mult, ALU.add)
-                nc.sync.dma_start(out=out[mb * P:(mb + 1) * P, cols], in_=result[:])
+        def term(name, mb, first=0, width=V, half=0.5):
+            d = "ab".index(name)
+            terms[name, mb, first] = held([P, width], F32, "term_%s%d_%d" % (name, mb, first))
+            nc.vector.scalar_tensor_tensor(terms[name, mb, first][:], gates[name, mb, first][:], half,
+                                           sampled[mb, d][:, first:first + width], ALU.subtract, ALU.mult)
+
+        def finish(mb, first=0, width=V):
+            result = held([P, width], F32, "result%d_%d" % (mb, first))
+            nc.vector.tensor_tensor(result[:], terms["a", mb, 0][:, first:first + width], terms["b", mb, first][:], ALU.add)
+            nc.sync.dma_start(out=out[mb * P:(mb + 1) * P, first:first + width], in_=result[:])
+            terms["sum", mb, first] = result
+
+
+        nc.vector.memset(planes[:].bitcast(I32), 0)
+        nc.gpsimd.memset(zero[:], 0.0)
+        nc.scalar.activation(centre[:], zero[:], ACT.Sigmoid)
+        nc.sync.dma_start(offs_t[:], offs)
+        load_words(0)
+        load_scales(nc.sync)
+        load_weights("y", 0)
+        load_weights("y", 1)
+        load_words(1)
+        load_weights("a", 0)
+        load_weights("a", 1)
+        nc.sync.dma_start(cen_t[:], cen)
+        load_weights("b", 0)
+        load_weights("b", 1)
+        nc.sync.dma_start(pos_t[0][:], pos1)
+        nc.sync.dma_start(pos_t[1][:], pos2)
 
         by_block = [(mb, h) for mb in range(BLOCKS) for h in range(HALVES)]
         by_half = [(mb, h) for h in range(HALVES) for mb in range(BLOCKS)]
-
-        nc.vector.memset(planes[:].bitcast(I32), 0)
-        nc.vector.memset(warm_in[:], 0.0)
-        nc.sync.dma_start(offs_t[:], offs)
-        nc.sync.dma_start(cen_t[:], cen)
-        nc.scalar.activation(warm_out[:], warm_in[:], ACT.Sigmoid)
-        for q in range(4):
-            nc.sync.dma_start(out=planes[32 * q:32 * q + PASSES * 4, :].bitcast(I32),
-                              in_=x_scales[:, 4 * q:4 * q + 4, :].bitcast(I32))
-        load_words(0)
-        load_weights("y", 0)
-        load_words(1)
-        load_weights("y", 1)
-        load_weights("a", 0)
-        nc.sync.dma_start(pos_t[0][:], pos1)
-        load_weights("b", 0)
-        load_weights("a", 1)
-        load_weights("b", 1)
-        nc.sync.dma_start(pos_t[1][:], pos2)
-
-        nc.vector.tensor_copy(x_planes[:], planes[:].indirect(offs_t[:]))
         gather_words(0, 0, HALVES)
-        prepare("y", 0)
-        multiply("y", 0, 0, by_block)
+        gather_scales(0, 1)
+        interleave(nc.scalar.copy, "y", 0)
+        quantize("y", 0)
+        gather_scales(1, 1, "rounded_y0")
+        for mb, h in by_half:
+            multiply("y", 0, 0, mb, h)
+        interleave(nc.scalar.copy, "y", 1)
+        quantize("y", 1)
         for h in range(HALVES):
             gather_words(1, h, 1)
-        prepare("y", 1)
-        multiply("y", 1, 0, by_block)
-        prepare("a", 0)
-        multiply("a", 0, 4, by_block)
-        evacuate([nc.vector.tensor_copy, nc.scalar.copy], "y", 0)
-        evacuate([nc.scalar.copy, nc.scalar.copy], "y", 1)
-        sample(0, 0, held([P, V], F32, "sampled00")[:])
-        prepare("b", 0, nc.vector.tensor_copy)
-        multiply("b", 0, 0, by_block)
-        prepare("a", 1)
-        multiply("a", 1, 4, by_block)
-        sample(1, 0, held([P, V], F32, "sampled10", "rounded_a1")[:])
-        prepare("b", 1)
-        multiply("b", 1, 0, by_block)
-        second_tap = held([P, BLOCKS, V], F32, "second_tap", "rounded_b1")
+        for mb, h in by_half:
+            multiply("y", 1, 0, mb, h)
+        interleave(nc.scalar.copy, "a", 0)
+        interleave(nc.vector.tensor_copy, "a", 1)
+        for o in range(PASSES):
+            quantize("a", o)
+            for mb, h in by_block:
+                multiply("a", o, 4, mb, h)
+        y_rows = held([P, BLOCKS * S], F32, "y_rows", "raw_a0")
         for mb in range(BLOCKS):
-            sample(mb, 1, second_tap[:, mb, :])
+            rows["y", mb] = y_rows[:, mb * S:(mb + 1) * S]
+        for mb, h in by_half:
+            evacuate(doubled, "y", mb, h)
+        interleave(nc.scalar.copy, "b", 0, True)
+        interleave(nc.vector.tensor_copy, "b", 1, True)
+        quantize("b", 0, PASSES)
+        for mb, h in by_block:
+            for o in range(PASSES):
+                multiply("b", o, 0, mb, h)
         for mb in range(BLOCKS):
-            evacuate([tanh, tanh], "a", mb)
-            first_term(mb)
-        for mb in range(BLOCKS):
-            evacuate([nc.scalar.copy, nc.scalar.copy], "b", mb)
-            finish(mb, 1 + mb)
+            for d in range(2):
+                sample(mb, d)
+
+        for h in range(HALVES):
+            evacuate(nc.scalar.copy, "a", 0, h)
+        gate("a", 0)
+        for h in range(HALVES):
+            evacuate(nc.scalar.copy, "b", 0, h)
+        gate("b", 0)
+        for h in range(HALVES):
+            evacuate(nc.scalar.copy, "a", 1, h)
+            evacuate(nc.vector.tensor_copy, "b", 1, h)
+        gate("a", 1)
+        pieces = [(0, 384), (384, 128)]
+        for first, width in pieces:
+            gate("b", 1, first, width)
+        term("a", 0, half=centre[:])
+        term("b", 0)
+        finish(0)
+        term("a", 1)
+        for first, width in pieces:
+            term("b", 1, first, width)
+        for first, width in pieces:
+            finish(1, first, width)

@@ -54,18 +54,19 @@ def tile_picked_zmodd_tanh_p_kernel(tc, x_words, x_scales, w0, w1, w2, offs, cen
         def load_words(o):
             nc.sync.dma_start(out=words[o][:].bitcast(I32), in_=x_words[o].rearrange("p n t -> p (n t)").bitcast(I32))
 
-        def load_scales(queue):
-            for q in range(4):
+        def load_scales(queue, quadrants):
+            for q in quadrants:
                 queue.dma_start(out=planes[32 * q:32 * q + PASSES * 4, :].bitcast(I32),
                                 in_=x_scales[:, 4 * q:4 * q + 4, :].bitcast(I32))
 
-        def interleave(copy, name, o, joint=False):
+        def interleave(copy, name, o, joint=False, cols=slice(0, N)):
             first = 0 if joint else o
-            if o == first:
+            if (name, first) not in rounded:
                 rounded[name, first] = held([P, (PASSES if joint else 1) * N * PACK], BF16, "rounded_%s%d" % (name, first))
-            dst = rounded[name, first][:, (o - first) * N * PACK:(o - first + 1) * N * PACK]
+            base = (o - first) * N * PACK
+            dst = rounded[name, first][:, base + cols.start * PACK:base + cols.stop * PACK]
             copy(out=dst.rearrange("p (c i t) -> p c t i", i=2, t=PACK),
-                 in_=raw[name, o][:].rearrange("p t (c i) -> p c t i", i=2))
+                 in_=raw[name, o][:, :, cols].rearrange("p t (c i) -> p c t i", i=2))
 
         def quantize(name, first, count=1):
             codes = held([P, count * N], U32, "w_codes_%s%d" % (name, first))
@@ -104,10 +105,10 @@ def tile_picked_zmodd_tanh_p_kernel(tc, x_words, x_scales, w0, w1, w2, offs, cen
                 stop=(o == PASSES - 1),
             )
 
-        def evacuate(emit, name, mb, h):
+        def evacuate(emit, name, mb, h, first=0, width=HALF):
             if (name, mb) not in rows:
                 rows[name, mb] = held([P, S], F32, "rows_%s%d" % (name, mb))[:]
-            emit(rows[name, mb][:, h * HALF:(h + 1) * HALF], banks[name, mb, h][:])
+            emit(rows[name, mb][:, h * HALF + first:h * HALF + first + width], banks[name, mb, h][:, first:first + width])
 
         def doubled(dst, src):
             nc.scalar.activation(dst, src, ACT.Copy, scale=2.0)
@@ -118,99 +119,107 @@ def tile_picked_zmodd_tanh_p_kernel(tc, x_words, x_scales, w0, w1, w2, offs, cen
         def tanh(dst, src):
             nc.scalar.activation(dst, src, ACT.Tanh)
 
-        def sample(mb, d, slot=None):
-            sampled[mb, d] = held([P, V], F32, "sampled%d%d" % (mb, d), slot)
-            nc.vector.tensor_copy(sampled[mb, d][:], rows["y", mb].indirect(pos_t[d][:]))
+        def sample(mb, d, dst):
+            sampled[mb, d] = dst
+            nc.vector.tensor_copy(dst, rows["y", mb].indirect(pos_t[d][:]))
 
         def gate(name, mb, first=0, width=V):
             gates[name, mb, first] = held([P, width], F32, "gate_%s%d_%d" % (name, mb, first))
             entries = cen_t[:, first // 16:(first + width) // 16]
             nc.scalar.activation(gates[name, mb, first][:], rows[name, mb].indirect(entries), ACT.Sigmoid, scale=2.0)
 
-        def term(name, mb, first=0, width=V, half=0.5):
+        def term(name, mb, first=0, width=V, half=0.5, slot=None):
             d = "ab".index(name)
-            terms[name, mb, first] = held([P, width], F32, "term_%s%d_%d" % (name, mb, first))
+            terms[name, mb, first] = held([P, width], F32, "term_%s%d_%d" % (name, mb, first), slot)
             nc.vector.scalar_tensor_tensor(terms[name, mb, first][:], gates[name, mb, first][:], half,
                                            sampled[mb, d][:, first:first + width], ALU.subtract, ALU.mult)
 
-        def finish(mb, first=0, width=V):
+        def masked(name, mb):
+            d = "ab".index(name)
+            terms[name, mb, 0] = held([P, V], F32, "term_%s%d_0" % (name, mb))
+            nc.vector.tensor_tensor(terms[name, mb, 0][:], rows[name, mb].indirect(cen_t[:]), sampled[mb, d], ALU.mult)
+
+        def centred(name, mb):
+            d = "ab".index(name)
+            below = held([P, V], F32, "below_%s%d" % (name, mb))
+            nc.scalar.activation(below[:], gates[name, mb, 0][:], ACT.Identity, scale=-1.0, bias=centre[:])
+            terms[name, mb, 0] = held([P, V], F32, "term_%s%d_0" % (name, mb))
+            nc.vector.tensor_tensor(terms[name, mb, 0][:], rows["y", mb].indirect(pos_t[d][:]), below[:], ALU.mult)
+
+        def finish(mb, scaled, weight, plain, first=0):
+            width = scaled.shape[1]
             result = held([P, width], F32, "result%d_%d" % (mb, first))
-            nc.vector.tensor_tensor(result[:], terms["a", mb, 0][:, first:first + width], terms["b", mb, first][:], ALU.add)
+            nc.vector.scalar_tensor_tensor(result[:], scaled, weight, plain, ALU.mult, ALU.add)
             nc.sync.dma_start(out=out[mb * P:(mb + 1) * P, first:first + width], in_=result[:])
             terms["sum", mb, first] = result
 
 
-        nc.vector.memset(planes[:].bitcast(I32), 0)
+        nc.vector.memset(planes[:, :T // 2].bitcast(I32), 0)
+        nc.gpsimd.memset(planes[:, T // 2:].bitcast(I32), 0)
         nc.gpsimd.memset(zero[:], 0.0)
         nc.scalar.activation(centre[:], zero[:], ACT.Sigmoid)
         nc.sync.dma_start(offs_t[:], offs)
+        load_scales(nc.sync, range(4))
         load_words(0)
-        load_scales(nc.sync)
         load_weights("y", 0)
-        load_weights("y", 1)
         load_words(1)
+        load_weights("y", 1)
         load_weights("a", 0)
         load_weights("a", 1)
-        nc.sync.dma_start(cen_t[:], cen)
         load_weights("b", 0)
-        load_weights("b", 1)
         nc.sync.dma_start(pos_t[0][:], pos1)
+        load_weights("b", 1)
+        nc.sync.dma_start(cen_t[:], cen)
         nc.sync.dma_start(pos_t[1][:], pos2)
 
         by_block = [(mb, h) for mb in range(BLOCKS) for h in range(HALVES)]
-        by_half = [(mb, h) for h in range(HALVES) for mb in range(BLOCKS)]
+        gather_scales(0, HALVES)
         gather_words(0, 0, HALVES)
-        gather_scales(0, 1)
         interleave(nc.scalar.copy, "y", 0)
         quantize("y", 0)
-        gather_scales(1, 1, "rounded_y0")
-        for mb, h in by_half:
+        for mb, h in by_block:
             multiply("y", 0, 0, mb, h)
+        gather_words(1, 0, HALVES)
         interleave(nc.scalar.copy, "y", 1)
         quantize("y", 1)
-        for h in range(HALVES):
-            gather_words(1, h, 1)
-        for mb, h in by_half:
+        for mb, h in by_block:
             multiply("y", 1, 0, mb, h)
         interleave(nc.scalar.copy, "a", 0)
         interleave(nc.vector.tensor_copy, "a", 1)
         for o in range(PASSES):
             quantize("a", o)
-            for mb, h in by_block:
-                multiply("a", o, 4, mb, h)
-        y_rows = held([P, BLOCKS * S], F32, "y_rows", "raw_a0")
         for mb in range(BLOCKS):
-            rows["y", mb] = y_rows[:, mb * S:(mb + 1) * S]
-        for mb, h in by_half:
-            evacuate(doubled, "y", mb, h)
-        interleave(nc.scalar.copy, "b", 0, True)
-        interleave(nc.vector.tensor_copy, "b", 1, True)
-        quantize("b", 0, PASSES)
-        for mb, h in by_block:
             for o in range(PASSES):
+                for h in range(HALVES):
+                    multiply("a", o, 4, mb, h)
+        for mb, h in by_block:
+            evacuate(doubled, "y", mb, h)
+        for o in range(PASSES):
+            interleave(nc.vector.tensor_copy, "b", o)
+            quantize("b", o)
+            for mb, h in by_block:
                 multiply("b", o, 0, mb, h)
-        for mb in range(BLOCKS):
-            for d in range(2):
-                sample(mb, d)
+        for d in range(2):
+            for mb in range(BLOCKS):
+                sample(mb, d, held([P, V], F32, "sampled%d%d" % (mb, d))[:])
 
-        for h in range(HALVES):
-            evacuate(nc.scalar.copy, "a", 0, h)
-        gate("a", 0)
+        for mb in range(BLOCKS):
+            for h in range(HALVES):
+                evacuate(nc.scalar.copy, "a", mb, h)
+            gate("a", mb)
         for h in range(HALVES):
             evacuate(nc.scalar.copy, "b", 0, h)
         gate("b", 0)
-        for h in range(HALVES):
-            evacuate(nc.scalar.copy, "a", 1, h)
-            evacuate(nc.vector.tensor_copy, "b", 1, h)
-        gate("a", 1)
+        evacuate(nc.vector.tensor_copy, "b", 1, 0)
+        evacuate(nc.scalar.copy, "b", 1, 1)
         pieces = [(0, 384), (384, 128)]
         for first, width in pieces:
             gate("b", 1, first, width)
         term("a", 0, half=centre[:])
-        term("b", 0)
-        finish(0)
         term("a", 1)
+        term("b", 0)
+        finish(0, terms["b", 0, 0][:], 1.0, terms["a", 0, 0][:])
         for first, width in pieces:
             term("b", 1, first, width)
         for first, width in pieces:
-            finish(1, first, width)
+            finish(1, terms["b", 1, first][:], 1.0, terms["a", 1, 0][:, first:first + width], first)

@@ -22,6 +22,7 @@ PASSES = K // K_PASS
 HALF = 512
 HALVES = S // HALF
 BLOCKS = N // P
+QUADRANTS = 4
 
 
 def tile_picked_zmodd_tanh_p_kernel(tc, x_words, x_scales, w0, w1, w2, offs, cen, pos1, pos2, out):
@@ -33,18 +34,16 @@ def tile_picked_zmodd_tanh_p_kernel(tc, x_words, x_scales, w0, w1, w2, offs, cen
 
         offs_t = lists.tile([P, S // 16], U16, name="offs_t")
         cen_t = lists.tile([P, V // 16], U16, name="cen_t")
-        pos_t = [lists.tile([P, V // 16], U16, name="pos_t%d" % d) for d in range(2)]
+        pos_t = {"a": lists.tile([P, V // 16], U16, name="pos1_t"), "b": lists.tile([P, V // 16], U16, name="pos2_t")}
 
         def held(shape, dtype, name, slot=None):
             return keep.tile(shape, dtype, name=name, tag=slot or name, align_bytes=64)
 
         weights = {"y": w0, "a": w1, "b": w2}
-        raw, rounded, w_codes, w_scales, x_codes, banks, rows, sampled, gates, terms = {}, {}, {}, {}, {}, {}, {}, {}, {}, {}
+        raw, rounded, w_codes, w_scales, x_codes, banks, rows, gates, terms = {}, {}, {}, {}, {}, {}, {}, {}, {}
         words = [held([P, T], U32, "words%d" % o) for o in range(PASSES)]
         planes = held([P, T], U8, "planes")
-        x_planes = {}
-        zero = held([P, 1], F32, "zero")
-        centre = held([P, 1], F32, "centre")
+        picked_planes = held([P, S], U8, "picked_planes")
 
         def load_weights(name, o):
             raw[name, o] = held([P, PACK, N], F32, "raw_%s%d" % (name, o))
@@ -54,12 +53,13 @@ def tile_picked_zmodd_tanh_p_kernel(tc, x_words, x_scales, w0, w1, w2, offs, cen
         def load_words(o):
             nc.sync.dma_start(out=words[o][:].bitcast(I32), in_=x_words[o].rearrange("p n t -> p (n t)").bitcast(I32))
 
-        def load_scales(queue, quadrants):
-            for q in quadrants:
-                queue.dma_start(out=planes[32 * q:32 * q + PASSES * 4, :].bitcast(I32),
-                                in_=x_scales[:, 4 * q:4 * q + 4, :].bitcast(I32))
+        def on_scalar(out, in_):
+            nc.scalar.activation(out, in_, ACT.Copy)
 
-        def interleave(copy, name, o, joint=False, cols=slice(0, N)):
+        def tanh(out, in_):
+            nc.scalar.activation(out, in_, ACT.Tanh)
+
+        def interleave(copy, name, o, cols=slice(0, N), joint=False):
             first = 0 if joint else o
             if (name, first) not in rounded:
                 rounded[name, first] = held([P, (PASSES if joint else 1) * N * PACK], BF16, "rounded_%s%d" % (name, first))
@@ -76,150 +76,111 @@ def tile_picked_zmodd_tanh_p_kernel(tc, x_words, x_scales, w0, w1, w2, offs, cen
                 w_codes[name, first + j] = codes[:, j * N:(j + 1) * N]
                 w_scales[name, first + j] = scales[:, j * N:(j + 1) * N]
 
-        def gather_scales(first, count, slot=None):
-            picked = held([P, count * HALF], U8, "x_planes%d" % first, slot)
-            cols = slice(first * HALF // 16, (first + count) * HALF // 16)
-            nc.vector.tensor_copy(picked[:], planes[:].indirect(offs_t[:, cols]))
-            for h in range(count):
-                x_planes[first + h] = picked[:, h * HALF:(h + 1) * HALF]
-
-        def gather_words(o, first, count, slot=None):
-            picked = held([P, count * HALF], U32, "x_codes%d%d" % (o, first), slot)
-            cols = slice(first * HALF // 16, (first + count) * HALF // 16)
-            nc.vector.tensor_copy(picked[:], words[o][:].indirect(offs_t[:, cols]))
-            for h in range(count):
-                x_codes[o, first + h] = picked[:, h * HALF:(h + 1) * HALF]
+        def gather_words(o):
+            x_codes[o] = held([P, S], U32, "x_codes%d" % o, "rounded_a%d" % (o - 1) if o else None)
+            nc.vector.tensor_copy(x_codes[o][:], words[o][:].indirect(offs_t[:]))
 
         def multiply(name, o, first_bank, mb, h):
             if o == 0:
                 tag = "bank%d" % (first_bank + mb * HALVES + h)
                 banks[name, mb, h] = psum.tile([P, HALF], F32, name=tag, tag=tag)
             m_cols = slice(mb * P, (mb + 1) * P)
+            s_cols = slice(h * HALF, (h + 1) * HALF)
             nc.tensor.matmul_mx(
                 out=banks[name, mb, h][:],
                 lhsT=w_codes[name, o][:, m_cols].bitcast(FP8X4),
                 lhsT_scale=w_scales[name, o][:, m_cols],
-                rhs=x_codes[o, h].bitcast(FP8X4),
-                rhs_scale=x_planes[h][PACK * o:P, :],
+                rhs=x_codes[o][:, s_cols].bitcast(FP8X4),
+                rhs_scale=x_planes[PACK * o:P, s_cols],
                 start=(o == 0),
                 stop=(o == PASSES - 1),
             )
 
-        def evacuate(emit, name, mb, h, first=0, width=HALF):
+        def evacuate(emit, name, mb, h, slot=None, first=0, width=HALF):
             if (name, mb) not in rows:
-                rows[name, mb] = held([P, S], F32, "rows_%s%d" % (name, mb))[:]
-            emit(rows[name, mb][:, h * HALF + first:h * HALF + first + width], banks[name, mb, h][:, first:first + width])
+                rows[name, mb] = held([P, S], F32, "rows_%s%d" % (name, mb), slot)
+            emit(out=rows[name, mb][:, h * HALF + first:h * HALF + first + width], in_=banks[name, mb, h][:, first:first + width])
 
-        def doubled(dst, src):
-            nc.scalar.activation(dst, src, ACT.Copy, scale=2.0)
+        def looked_up(name, mb, factor, first, width):
+            window, entries = (rows[name, mb], cen_t) if factor == "mask" else (rows["y", mb], pos_t[name])
+            return window[:].indirect(entries[:, first // 16:(first + width) // 16])
 
-        def doubled_v(dst, src):
-            nc.vector.tensor_scalar(dst, src, 2.0, None, ALU.mult)
+        def gate(name, mb, factor, first=0, width=V, slot=None):
+            gates[name, mb, first] = held([P, width], F32, "gate_%s%d_%d" % (name, mb, first), slot)
+            on_scalar(gates[name, mb, first][:], looked_up(name, mb, factor, first, width))
 
-        def tanh(dst, src):
-            nc.scalar.activation(dst, src, ACT.Tanh)
-
-        def sample(mb, d, dst):
-            sampled[mb, d] = dst
-            nc.vector.tensor_copy(dst, rows["y", mb].indirect(pos_t[d][:]))
-
-        def gate(name, mb, first=0, width=V):
-            gates[name, mb, first] = held([P, width], F32, "gate_%s%d_%d" % (name, mb, first))
-            entries = cen_t[:, first // 16:(first + width) // 16]
-            nc.scalar.activation(gates[name, mb, first][:], rows[name, mb].indirect(entries), ACT.Sigmoid, scale=2.0)
-
-        def term(name, mb, first=0, width=V, half=0.5, slot=None):
-            d = "ab".index(name)
+        def term(name, mb, factor, first=0, width=V, slot=None):
             terms[name, mb, first] = held([P, width], F32, "term_%s%d_%d" % (name, mb, first), slot)
-            nc.vector.scalar_tensor_tensor(terms[name, mb, first][:], gates[name, mb, first][:], half,
-                                           sampled[mb, d][:, first:first + width], ALU.subtract, ALU.mult)
+            nc.vector.tensor_tensor(terms[name, mb, first][:], looked_up(name, mb, factor, first, width), gates[name, mb, first][:], ALU.mult)
 
-        def masked(name, mb):
-            d = "ab".index(name)
-            terms[name, mb, 0] = held([P, V], F32, "term_%s%d_0" % (name, mb))
-            nc.vector.tensor_tensor(terms[name, mb, 0][:], rows[name, mb].indirect(cen_t[:]), sampled[mb, d], ALU.mult)
-
-        def centred(name, mb):
-            d = "ab".index(name)
-            below = held([P, V], F32, "below_%s%d" % (name, mb))
-            nc.scalar.activation(below[:], gates[name, mb, 0][:], ACT.Identity, scale=-1.0, bias=centre[:])
-            terms[name, mb, 0] = held([P, V], F32, "term_%s%d_0" % (name, mb))
-            nc.vector.tensor_tensor(terms[name, mb, 0][:], rows["y", mb].indirect(pos_t[d][:]), below[:], ALU.mult)
-
-        def finish(mb, scaled, weight, plain, first=0):
-            width = scaled.shape[1]
+        def finish(mb, first=0, width=V):
             result = held([P, width], F32, "result%d_%d" % (mb, first))
-            nc.vector.scalar_tensor_tensor(result[:], scaled, weight, plain, ALU.mult, ALU.add)
+            nc.vector.tensor_tensor(result[:], terms["b", mb, first][:], terms["a", mb, 0][:, first:first + width], ALU.add)
             nc.sync.dma_start(out=out[mb * P:(mb + 1) * P, first:first + width], in_=result[:])
-            terms["sum", mb, first] = result
 
-
-        nc.vector.memset(planes[:, :T // 2].bitcast(I32), 0)
-        nc.gpsimd.memset(planes[:, T // 2:].bitcast(I32), 0)
-        nc.gpsimd.memset(zero[:], 0.0)
-        nc.scalar.activation(centre[:], zero[:], ACT.Sigmoid)
+        x_planes = held([P, S], U8, "x_planes")
+        live = PASSES * 4
         nc.sync.dma_start(offs_t[:], offs)
-        load_scales(nc.sync, range(4))
+        for r in range(4):
+            nc.sync.dma_start(out=planes[r:QUADRANTS * live:4, :].bitcast(I32),
+                              in_=x_scales.rearrange("o (q r) c -> r q o c", r=4)[r].bitcast(I32))
+        nc.vector.memset(planes[32:64, :].bitcast(I32), 0)
+        nc.gpsimd.memset(planes[64:P, :].bitcast(I32), 0)
+        nc.vector.memset(x_planes[:].bitcast(I32), 0)
         load_words(0)
-        load_weights("y", 0)
-        load_words(1)
-        load_weights("y", 1)
         load_weights("a", 0)
+        load_words(1)
+        nc.vector.tensor_copy(picked_planes[:], planes[:].indirect(offs_t[:]))
+        for q in range(QUADRANTS):
+            nc.sync.dma_start(out=x_planes[32 * q:32 * q + live, :].bitcast(I32), in_=picked_planes[live * q:live * (q + 1), :].bitcast(I32))
         load_weights("a", 1)
-        load_weights("b", 0)
-        nc.sync.dma_start(pos_t[0][:], pos1)
-        load_weights("b", 1)
+        load_weights("y", 0)
         nc.sync.dma_start(cen_t[:], cen)
-        nc.sync.dma_start(pos_t[1][:], pos2)
+        load_weights("y", 1)
+        load_weights("b", 0)
+        load_weights("b", 1)
+        nc.sync.dma_start(pos_t["a"][:], pos1)
+        nc.sync.dma_start(pos_t["b"][:], pos2)
 
         by_block = [(mb, h) for mb in range(BLOCKS) for h in range(HALVES)]
-        gather_scales(0, HALVES)
-        gather_words(0, 0, HALVES)
-        interleave(nc.scalar.copy, "y", 0)
-        quantize("y", 0)
-        for mb, h in by_block:
-            multiply("y", 0, 0, mb, h)
-        gather_words(1, 0, HALVES)
-        interleave(nc.scalar.copy, "y", 1)
-        quantize("y", 1)
-        for mb, h in by_block:
-            multiply("y", 1, 0, mb, h)
-        interleave(nc.scalar.copy, "a", 0)
-        interleave(nc.vector.tensor_copy, "a", 1)
         for o in range(PASSES):
+            gather_words(o)
+            interleave(on_scalar, "a", o)
             quantize("a", o)
-        for mb in range(BLOCKS):
-            for o in range(PASSES):
-                for h in range(HALVES):
-                    multiply("a", o, 4, mb, h)
-        for mb, h in by_block:
-            evacuate(doubled, "y", mb, h)
-        for o in range(PASSES):
-            interleave(nc.vector.tensor_copy, "b", o)
-            quantize("b", o)
             for mb, h in by_block:
-                multiply("b", o, 0, mb, h)
-        for d in range(2):
-            for mb in range(BLOCKS):
-                sample(mb, d, held([P, V], F32, "sampled%d%d" % (mb, d))[:])
-
-        for mb in range(BLOCKS):
-            for h in range(HALVES):
-                evacuate(nc.scalar.copy, "a", mb, h)
-            gate("a", mb)
+                multiply("a", o, 0, mb, h)
+        interleave(on_scalar, "y", 0, slice(0, P), joint=True)
+        interleave(nc.vector.tensor_copy, "y", 0, slice(P, N), joint=True)
+        interleave(nc.vector.tensor_copy, "y", 1, joint=True)
+        quantize("y", 0, PASSES)
+        by_bank = [(mb, h, o) for mb, h in by_block for o in range(PASSES)]
+        for mb, h, o in by_bank:
+            multiply("y", o, 4, mb, h)
+        for mb, h in by_block:
+            evacuate(tanh, "a", mb, h)
+        for o in range(PASSES):
+            interleave(nc.vector.tensor_copy, "b", o, joint=True)
+        quantize("b", 0, PASSES)
+        for mb, h, o in by_bank:
+            multiply("b", o, 0, mb, h)
+        evacuate(on_scalar, "y", 0, 0, "raw_b1")
+        for mb, h in by_block[1:]:
+            evacuate(nc.vector.tensor_copy, "y", mb, h, "rounded_b0")
+        gate("a", 0, "mask")
+        gate("a", 1, "mask", slot="w_codes_y0")
         for h in range(HALVES):
-            evacuate(nc.scalar.copy, "b", 0, h)
-        gate("b", 0)
-        evacuate(nc.vector.tensor_copy, "b", 1, 0)
-        evacuate(nc.scalar.copy, "b", 1, 1)
-        pieces = [(0, 384), (384, 128)]
+            evacuate(tanh, "b", 0, h)
+        gate("b", 0, "sample")
+        for h in range(HALVES):
+            evacuate(tanh, "b", 1, h)
+        pieces = [(0, 256), (256, 256)]
         for first, width in pieces:
-            gate("b", 1, first, width)
-        term("a", 0, half=centre[:])
-        term("a", 1)
-        term("b", 0)
-        finish(0, terms["b", 0, 0][:], 1.0, terms["a", 0, 0][:])
+            gate("b", 1, "sample", first, width)
+        term("a", 0, "sample")
+        term("a", 1, "sample")
+        term("b", 0, "mask")
+        finish(0)
         for first, width in pieces:
-            term("b", 1, first, width)
+            term("b", 1, "mask", first, width)
         for first, width in pieces:
-            finish(1, terms["b", 1, first][:], 1.0, terms["a", 1, 0][:, first:first + width], first)
+            finish(1, first, width)

@@ -59,39 +59,39 @@ def tile_picked_zmodd_tanh_p_kernel(tc, x_words, x_scales, w0, w1, w2, offs, cen
         def tanh(out, in_):
             nc.scalar.activation(out, in_, ACT.Tanh)
 
-        def interleave(copy, name, o, cols=slice(0, N), joint=False):
-            first = 0 if joint else o
-            if (name, first) not in rounded:
-                rounded[name, first] = held([P, (PASSES if joint else 1) * N * PACK], BF16, "rounded_%s%d" % (name, first))
-            base = (o - first) * N * PACK
-            dst = rounded[name, first][:, base + cols.start * PACK:base + cols.stop * PACK]
-            copy(out=dst.rearrange("p (c i t) -> p c t i", i=2, t=PACK),
-                 in_=raw[name, o][:, :, cols].rearrange("p t (c i) -> p c t i", i=2))
-
-        def quantize(name, first, count=1):
-            codes = held([P, count * N], U32, "w_codes_%s%d" % (name, first))
-            scales = held([P, count * N], U8, "w_scales_%s%d" % (name, first))
-            nc.vector.quantize_mx(out=codes[:].bitcast(FP8X4), scales=scales[:], in_=rounded[name, first][:])
+        def stage(name, first, count):
+            tile = held([P, count * P * PACK], BF16, "rounded_%s%d" % (name, first))
             for j in range(count):
-                w_codes[name, first + j] = codes[:, j * N:(j + 1) * N]
-                w_scales[name, first + j] = scales[:, j * N:(j + 1) * N]
+                rounded[name, first + j] = tile[:, j * P * PACK:]
+
+        def interleave(copy, name, o, mb=0, count=BLOCKS):
+            copy(out=rounded[name, o * BLOCKS + mb][:, :count * P * PACK].rearrange("p (c i t) -> p c t i", i=2, t=PACK),
+                 in_=raw[name, o][:, :, mb * P:(mb + count) * P].rearrange("p t (c i) -> p c t i", i=2))
+
+        def quantize(name, first, count):
+            codes = held([P, count * P], U32, "w_codes_%s%d" % (name, first))
+            scales = held([P, count * P], U8, "w_scales_%s%d" % (name, first))
+            nc.vector.quantize_mx(out=codes[:].bitcast(FP8X4), scales=scales[:], in_=rounded[name, first][:, :count * P * PACK])
+            for j in range(count):
+                o, mb = divmod(first + j, BLOCKS)
+                w_codes[name, o, mb] = codes[:, j * P:(j + 1) * P]
+                w_scales[name, o, mb] = scales[:, j * P:(j + 1) * P]
 
         def gather_words(o):
-            x_codes[o] = held([P, S], U32, "x_codes%d" % o, "rounded_a%d" % (o - 1) if o else None)
+            x_codes[o] = held([P, S], U32, "x_codes%d" % o, "rounded_a0" if o else None)
             nc.vector.tensor_copy(x_codes[o][:], words[o][:].indirect(offs_t[:]))
 
         def multiply(name, o, first_bank, mb, h):
             if o == 0:
                 tag = "bank%d" % (first_bank + mb * HALVES + h)
                 banks[name, mb, h] = psum.tile([P, HALF], F32, name=tag, tag=tag)
-            m_cols = slice(mb * P, (mb + 1) * P)
             s_cols = slice(h * HALF, (h + 1) * HALF)
             nc.tensor.matmul_mx(
                 out=banks[name, mb, h][:],
-                lhsT=w_codes[name, o][:, m_cols].bitcast(FP8X4),
-                lhsT_scale=w_scales[name, o][:, m_cols],
+                lhsT=w_codes[name, o, mb].bitcast(FP8X4),
+                lhsT_scale=w_scales[name, o, mb],
                 rhs=x_codes[o][:, s_cols].bitcast(FP8X4),
-                rhs_scale=x_planes[PACK * o:P, s_cols],
+                rhs_scale=x_planes[o][:, s_cols],
                 start=(o == 0),
                 stop=(o == PASSES - 1),
             )
@@ -118,23 +118,27 @@ def tile_picked_zmodd_tanh_p_kernel(tc, x_words, x_scales, w0, w1, w2, offs, cen
             nc.vector.tensor_tensor(result[:], terms["b", mb, first][:], terms["a", mb, 0][:, first:first + width], ALU.add)
             nc.sync.dma_start(out=out[mb * P:(mb + 1) * P, first:first + width], in_=result[:])
 
-        x_planes = held([P, S], U8, "x_planes")
-        live = PASSES * 4
+        x_planes = [held([P, S], U8, "x_planes%d" % o) for o in range(PASSES)]
+
+        def place_scales(o):
+            for q in range(QUADRANTS):
+                nc.sync.dma_start(out=x_planes[o][32 * q:32 * q + 4, :].bitcast(I32),
+                                  in_=picked_planes[16 * o + 4 * q:16 * o + 4 * q + 4, :].bitcast(I32))
+
         nc.sync.dma_start(offs_t[:], offs)
-        for r in range(4):
-            nc.sync.dma_start(out=planes[r:QUADRANTS * live:4, :].bitcast(I32),
-                              in_=x_scales.rearrange("o (q r) c -> r q o c", r=4)[r].bitcast(I32))
+        nc.sync.dma_start(out=planes[0:32, :].bitcast(I32), in_=x_scales.rearrange("o q c -> (o q) c").bitcast(I32))
         nc.vector.memset(planes[32:64, :].bitcast(I32), 0)
         nc.gpsimd.memset(planes[64:P, :].bitcast(I32), 0)
-        nc.vector.memset(x_planes[:].bitcast(I32), 0)
+        for o in range(PASSES):
+            nc.vector.memset(x_planes[o][:].bitcast(I32), 0)
         load_words(0)
         load_weights("a", 0)
         load_words(1)
         nc.vector.tensor_copy(picked_planes[:], planes[:].indirect(offs_t[:]))
-        for q in range(QUADRANTS):
-            nc.sync.dma_start(out=x_planes[32 * q:32 * q + live, :].bitcast(I32), in_=picked_planes[live * q:live * (q + 1), :].bitcast(I32))
+        place_scales(0)
         load_weights("a", 1)
         load_weights("y", 0)
+        place_scales(1)
         nc.sync.dma_start(cen_t[:], cen)
         load_weights("y", 1)
         load_weights("b", 0)
@@ -143,44 +147,58 @@ def tile_picked_zmodd_tanh_p_kernel(tc, x_words, x_scales, w0, w1, w2, offs, cen
         nc.sync.dma_start(pos_t["b"][:], pos2)
 
         by_block = [(mb, h) for mb in range(BLOCKS) for h in range(HALVES)]
-        for o in range(PASSES):
-            gather_words(o)
-            interleave(on_scalar, "a", o)
-            quantize("a", o)
-            for mb, h in by_block:
-                multiply("a", o, 0, mb, h)
-        interleave(on_scalar, "y", 0, slice(0, P), joint=True)
-        interleave(nc.vector.tensor_copy, "y", 0, slice(P, N), joint=True)
-        interleave(nc.vector.tensor_copy, "y", 1, joint=True)
-        quantize("y", 0, PASSES)
         by_bank = [(mb, h, o) for mb, h in by_block for o in range(PASSES)]
-        for mb, h, o in by_bank:
-            multiply("y", o, 4, mb, h)
+        gather_words(0)
+        stage("a", 0, BLOCKS)
+        interleave(on_scalar, "a", 0)
+        quantize("a", 0, BLOCKS)
+        for mb, h in by_block:
+            multiply("a", 0, 0, mb, h)
+        gather_words(1)
+        stage("a", BLOCKS, BLOCKS)
+        for mb in range(BLOCKS):
+            interleave(on_scalar, "a", 1, mb, 1)
+            quantize("a", BLOCKS + mb, 1)
+            for h in range(HALVES):
+                multiply("a", 1, 0, mb, h)
+
+        def last_pass(name, first_bank):
+            for mb in range(BLOCKS):
+                interleave(nc.vector.tensor_copy, name, 1, mb, 1)
+            quantize(name, 0, 3)
+            quantize(name, 3, 1)
+            for mb, h, o in by_bank:
+                multiply(name, o, first_bank, mb, h)
+
+        stage("y", 0, 3)
+        stage("y", 3, 1)
+        interleave(on_scalar, "y", 0, 0, 1)
+        interleave(nc.vector.tensor_copy, "y", 0, 1, 1)
+        last_pass("y", 4)
         for mb, h in by_block:
             evacuate(tanh, "a", mb, h)
-        for o in range(PASSES):
-            interleave(nc.vector.tensor_copy, "b", o, joint=True)
-        quantize("b", 0, PASSES)
-        for mb, h, o in by_bank:
-            multiply("b", o, 0, mb, h)
+        stage("b", 0, 3)
+        stage("b", 3, 1)
+        interleave(nc.vector.tensor_copy, "b", 0)
+        last_pass("b", 0)
         evacuate(on_scalar, "y", 0, 0, "raw_b1")
         for mb, h in by_block[1:]:
             evacuate(nc.vector.tensor_copy, "y", mb, h, "rounded_b0")
         gate("a", 0, "mask")
-        gate("a", 1, "mask", slot="w_codes_y0")
+        gate("a", 1, "mask", slot="rounded_b3")
         for h in range(HALVES):
             evacuate(tanh, "b", 0, h)
-        gate("b", 0, "sample")
+        pieces = [(0, 256), (256, 256)]
+        for first, width in pieces:
+            gate("b", 0, "sample", first, width)
         for h in range(HALVES):
             evacuate(tanh, "b", 1, h)
-        pieces = [(0, 256), (256, 256)]
         for first, width in pieces:
             gate("b", 1, "sample", first, width)
         term("a", 0, "sample")
         term("a", 1, "sample")
-        term("b", 0, "mask")
-        finish(0)
-        for first, width in pieces:
-            term("b", 1, "mask", first, width)
-        for first, width in pieces:
-            finish(1, first, width)
+        for mb in range(BLOCKS):
+            for first, width in pieces:
+                term("b", mb, "mask", first, width)
+            for first, width in pieces:
+                finish(mb, first, width)

@@ -40,7 +40,7 @@ def tile_picked_zmodd_tanh_p_kernel(tc, x_words, x_scales, w0, w1, w2, offs, cen
             return keep.tile(shape, dtype, name=name, tag=slot or name, align_bytes=64)
 
         weights = {"y": w0, "a": w1, "b": w2}
-        raw, rounded, w_codes, w_scales, x_codes, banks, rows, gates, terms = {}, {}, {}, {}, {}, {}, {}, {}, {}
+        raw, rounded, w_codes, w_scales, x_codes, banks, rows, gates, terms, results = {}, {}, {}, {}, {}, {}, {}, {}, {}, {}
         words = [held([P, T], U32, "words%d" % o) for o in range(PASSES)]
         planes = held([P, T], U8, "planes")
         picked_planes = held([P, S], U8, "picked_planes")
@@ -113,10 +113,13 @@ def tile_picked_zmodd_tanh_p_kernel(tc, x_words, x_scales, w0, w1, w2, offs, cen
             terms[name, mb, first] = held([P, width], F32, "term_%s%d_%d" % (name, mb, first), slot)
             nc.vector.tensor_tensor(terms[name, mb, first][:], looked_up(name, mb, factor, first, width), gates[name, mb, first][:], ALU.mult)
 
-        def finish(mb, first=0, width=V):
-            result = held([P, width], F32, "result%d_%d" % (mb, first))
-            nc.vector.tensor_tensor(result[:], terms["b", mb, first][:], terms["a", mb, 0][:, first:first + width], ALU.add)
-            nc.sync.dma_start(out=out[mb * P:(mb + 1) * P, first:first + width], in_=result[:])
+        def finish(mb, first, width):
+            if mb not in results:
+                results[mb] = held([P, V], F32, "result%d" % mb)
+            nc.vector.tensor_tensor(results[mb][:, first:first + width], terms["b", mb, first][:], terms["a", mb, 0][:, first:first + width], ALU.add)
+
+        def store(mb, first=0, width=V):
+            nc.sync.dma_start(out=out[mb * P:(mb + 1) * P, first:first + width], in_=results[mb][:, first:first + width])
 
         x_planes = [held([P, S], U8, "x_planes%d" % o) for o in range(PASSES)]
 
@@ -181,11 +184,11 @@ def tile_picked_zmodd_tanh_p_kernel(tc, x_words, x_scales, w0, w1, w2, offs, cen
         stage("b", 3, 1)
         interleave(nc.vector.tensor_copy, "b", 0)
         last_pass("b", 0)
-        evacuate(on_scalar, "y", 0, 0, "raw_b1")
-        for mb, h in by_block[1:]:
-            evacuate(nc.vector.tensor_copy, "y", mb, h, "rounded_b0")
-        gate("a", 0, "mask")
-        gate("a", 1, "mask", slot="rounded_b3")
+        for mb, h in by_block[:-1]:
+            evacuate(nc.vector.tensor_copy, "y", mb, h, ["raw_b1", "rounded_b0"][mb])
+        for mb in range(BLOCKS):
+            gate("a", mb, "mask")
+        evacuate(on_scalar, "y", 1, 1)
         for h in range(HALVES):
             evacuate(tanh, "b", 0, h)
         pieces = [(0, 256), (256, 256)]
@@ -197,8 +200,13 @@ def tile_picked_zmodd_tanh_p_kernel(tc, x_words, x_scales, w0, w1, w2, offs, cen
             gate("b", 1, "sample", first, width)
         term("a", 0, "sample")
         term("a", 1, "sample")
-        for mb in range(BLOCKS):
-            for first, width in pieces:
-                term("b", mb, "mask", first, width)
-            for first, width in pieces:
-                finish(mb, first, width)
+        for first, width in pieces:
+            term("b", 0, "mask", first, width)
+        for first, width in pieces:
+            finish(0, first, width)
+        store(0)
+        for first, width in pieces:
+            term("b", 1, "mask", first, width)
+        for first, width in pieces:
+            finish(1, first, width)
+            store(1, first, width)

@@ -175,8 +175,7 @@ def tile_picked_zmodd_tanh_p_kernel(tc, x_words, x_scales, w0, w1, w2, offs, cen
 
         stage("y", 0, 3)
         stage("y", 3, 1)
-        interleave(on_scalar, "y", 0, 0, 1)
-        interleave(nc.vector.tensor_copy, "y", 0, 1, 1)
+        interleave(nc.vector.tensor_copy, "y", 0)
         last_pass("y", 4)
         for mb, h in by_block:
             evacuate(tanh, "a", mb, h)

@@ -128,8 +128,8 @@ def tile_picked_zmodd_tanh_p_kernel(tc, x_words, x_scales, w0, w1, w2, offs, cen
                 nc.sync.dma_start(out=x_planes[o][32 * q:32 * q + 4, :].bitcast(I32),
                                   in_=picked_planes[16 * o + 4 * q:16 * o + 4 * q + 4, :].bitcast(I32))
 
-        nc.sync.dma_start(offs_t[:], offs)
         nc.sync.dma_start(out=planes[0:32, :].bitcast(I32), in_=x_scales.rearrange("o q c -> (o q) c").bitcast(I32))
+        nc.sync.dma_start(offs_t[:], offs)
         nc.vector.memset(planes[32:64, :].bitcast(I32), 0)
         nc.gpsimd.memset(planes[64:P, :].bitcast(I32), 0)
         for o in range(PASSES):

@@ -78,7 +78,7 @@ def tile_picked_zmodd_tanh_p_kernel(tc, x_words, x_scales, w0, w1, w2, offs, cen
                 w_scales[name, o, mb] = scales[:, j * P:(j + 1) * P]
 
         def gather_words(o):
-            x_codes[o] = held([P, S], U32, "x_codes%d" % o, "rounded_a0" if o else None)
+            x_codes[o] = held([P, S], U32, "x_codes%d" % o, "raw_a0" if o else None)
             nc.vector.tensor_copy(x_codes[o][:], words[o][:].indirect(offs_t[:]))
 
         def multiply(name, o, first_bank, mb, h):

@@ -37,7 +37,7 @@ def tile_picked_zmodd_tanh_p_kernel(tc, x_words, x_scales, w0, w1, w2, offs, cen
         pos_t = {"a": lists.tile([P, V // 16], U16, name="pos1_t"), "b": lists.tile([P, V // 16], U16, name="pos2_t")}
 
         def held(shape, dtype, name, slot=None):
-            return keep.tile(shape, dtype, name=name, tag=slot or name, align_bytes=64)
+            return keep.tile(shape, dtype, name=name, tag=slot or name, align_bytes=256)
 
         weights = {"y": w0, "a": w1, "b": w2}
         raw, rounded, w_codes, w_scales, x_codes, banks, rows, gates, terms, results = {}, {}, {}, {}, {}, {}, {}, {}, {}, {}

@@ -131,7 +131,7 @@ def tile_picked_zmodd_tanh_p_kernel(tc, x_words, x_scales, w0, w1, w2, offs, cen
         nc.sync.dma_start(out=planes[0:32, :].bitcast(I32), in_=x_scales.rearrange("o q c -> (o q) c").bitcast(I32))
         nc.sync.dma_start(offs_t[:], offs)
         nc.vector.memset(planes[32:64, :].bitcast(I32), 0)
-        nc.gpsimd.memset(planes[64:P, :].bitcast(I32), 0)
+        nc.vector.memset(planes[64:P, :].bitcast(I32), 0)
         for o in range(PASSES):
             nc.vector.memset(x_planes[o][:].bitcast(I32), 0)
         load_words(0)

from contextlib import ExitStack

import concourse.mybir as mybir

K, T, S, V, N = 1024, 2048, 1024, 512, 256
FLOPS = 3 * 2 * K * N * S

F32 = mybir.dt.float32
BF16 = mybir.dt.bfloat16
I32 = mybir.dt.int32
U32 = mybir.dt.uint32
U16 = mybir.dt.uint16
U8 = mybir.dt.uint8
FP8X4 = mybir.dt.float8_e4m3fn_x4
ACT = mybir.ActivationFunctionType
ALU = mybir.AluOpType

P = 128
PACK = 4
K_PASS = P * PACK
PASSES = K // K_PASS
HALF = 512
HALVES = S // HALF
BLOCKS = N // P
QUADRANTS = 4


def tile_picked_zmodd_tanh_p_kernel(tc, x_words, x_scales, w0, w1, w2, offs, cen, pos1, pos2, out):
    nc = tc.nc
    with ExitStack() as ctx:
        lists = ctx.enter_context(tc.tile_pool(name="lists", bufs=1))
        keep = ctx.enter_context(tc.tile_pool(name="keep", bufs=1))
        psum = ctx.enter_context(tc.psum_pool(name="psum", bufs=1))

        offs_t = lists.tile([P, S // 16], U16, name="offs_t")
        cen_t = lists.tile([P, V // 16], U16, name="cen_t")
        pos_t = {"a": lists.tile([P, V // 16], U16, name="pos1_t"), "b": lists.tile([P, V // 16], U16, name="pos2_t")}

        def held(shape, dtype, name, slot=None):
            return keep.tile(shape, dtype, name=name, tag=slot or name, align_bytes=256)

        weights = {"y": w0, "a": w1, "b": w2}
        raw, rounded, w_codes, w_scales, x_codes, banks, rows, gates, terms, results = {}, {}, {}, {}, {}, {}, {}, {}, {}, {}
        words = [held([P, T], U32, "words%d" % o) for o in range(PASSES)]
        planes = held([P, T], U8, "planes")
        picked_planes = held([P, S], U8, "picked_planes")

        def load_weights(name, o):
            raw[name, o] = held([P, PACK, N], F32, "raw_%s%d" % (name, o))
            k_rows = weights[name][o * K_PASS:(o + 1) * K_PASS, :]
            nc.sync.dma_start(out=raw[name, o][:], in_=k_rows.rearrange("(p j) w -> p j w", j=PACK))

        def load_words(o):
            nc.sync.dma_start(out=words[o][:].bitcast(I32), in_=x_words[o].rearrange("p n t -> p (n t)").bitcast(I32))

        def on_scalar(out, in_):
            nc.scalar.activation(out, in_, ACT.Copy)

        def tanh(out, in_):
            nc.scalar.activation(out, in_, ACT.Tanh)

        def stage(name, first, count):
            tile = held([P, count * P * PACK], BF16, "rounded_%s%d" % (name, first))
            for j in range(count):
                rounded[name, first + j] = tile[:, j * P * PACK:]

        def interleave(copy, name, o, mb=0, count=BLOCKS):
            copy(out=rounded[name, o * BLOCKS + mb][:, :count * P * PACK].rearrange("p (c i t) -> p c t i", i=2, t=PACK),
                 in_=raw[name, o][:, :, mb * P:(mb + count) * P].rearrange("p t (c i) -> p c t i", i=2))

        def quantize(name, first, count):
            codes = held([P, count * P], U32, "w_codes_%s%d" % (name, first))
            scales = held([P, count * P], U8, "w_scales_%s%d" % (name, first))
            nc.vector.quantize_mx(out=codes[:].bitcast(FP8X4), scales=scales[:], in_=rounded[name, first][:, :count * P * PACK])
            for j in range(count):
                o, mb = divmod(first + j, BLOCKS)
                w_codes[name, o, mb] = codes[:, j * P:(j + 1) * P]
                w_scales[name, o, mb] = scales[:, j * P:(j + 1) * P]

        def gather_words(o):
            x_codes[o] = held([P, S], U32, "x_codes%d" % o, "raw_a0" if o else None)
            nc.vector.tensor_copy(x_codes[o][:], words[o][:].indirect(offs_t[:]))

        def multiply(name, o, first_bank, mb, h):
            if o == 0:
                tag = "bank%d" % (first_bank + mb * HALVES + h)
                banks[name, mb, h] = psum.tile([P, HALF], F32, name=tag, tag=tag)
            s_cols = slice(h * HALF, (h + 1) * HALF)
            nc.tensor.matmul_mx(
                out=banks[name, mb, h][:],
                lhsT=w_codes[name, o, mb].bitcast(FP8X4),
                lhsT_scale=w_scales[name, o, mb],
                rhs=x_codes[o][:, s_cols].bitcast(FP8X4),
                rhs_scale=x_planes[o][:, s_cols],
                start=(o == 0),
                stop=(o == PASSES - 1),
            )

        def evacuate(emit, name, mb, h, slot=None, first=0, width=HALF):
            if (name, mb) not in rows:
                rows[name, mb] = held([P, S], F32, "rows_%s%d" % (name, mb), slot)
            emit(out=rows[name, mb][:, h * HALF + first:h * HALF + first + width], in_=banks[name, mb, h][:, first:first + width])

        def looked_up(name, mb, factor, first, width):
            window, entries = (rows[name, mb], cen_t) if factor == "mask" else (rows["y", mb], pos_t[name])
            return window[:].indirect(entries[:, first // 16:(first + width) // 16])

        def gate(name, mb, factor, first=0, width=V, slot=None):
            gates[name, mb, first] = held([P, width], F32, "gate_%s%d_%d" % (name, mb, first), slot)
            on_scalar(gates[name, mb, first][:], looked_up(name, mb, factor, first, width))

        def term(name, mb, factor, first=0, width=V, slot=None):
            terms[name, mb, first] = held([P, width], F32, "term_%s%d_%d" % (name, mb, first), slot)
            nc.vector.tensor_tensor(terms[name, mb, first][:], looked_up(name, mb, factor, first, width), gates[name, mb, first][:], ALU.mult)

        def finish(mb, first, width):
            if mb not in results:
                results[mb] = held([P, V], F32, "result%d" % mb)
            nc.vector.tensor_tensor(results[mb][:, first:first + width], terms["b", mb, first][:], terms["a", mb, 0][:, first:first + width], ALU.add)

        def store(mb, first=0, width=V):
            nc.sync.dma_start(out=out[mb * P:(mb + 1) * P, first:first + width], in_=results[mb][:, first:first + width])

        x_planes = [held([P, S], U8, "x_planes%d" % o) for o in range(PASSES)]

        def place_scales(o):
            for q in range(QUADRANTS):
                nc.sync.dma_start(out=x_planes[o][32 * q:32 * q + 4, :].bitcast(I32),
                                  in_=picked_planes[16 * o + 4 * q:16 * o + 4 * q + 4, :].bitcast(I32))

        nc.sync.dma_start(out=planes[0:32, :].bitcast(I32), in_=x_scales.rearrange("o q c -> (o q) c").bitcast(I32))
        nc.sync.dma_start(offs_t[:], offs)
        nc.vector.memset(planes[32:64, :].bitcast(I32), 0)
        nc.vector.memset(planes[64:P, :].bitcast(I32), 0)
        for o in range(PASSES):
            nc.vector.memset(x_planes[o][:].bitcast(I32), 0)
        load_words(0)
        load_weights("a", 0)
        load_words(1)
        nc.vector.tensor_copy(picked_planes[:], planes[:].indirect(offs_t[:]))
        place_scales(0)
        load_weights("a", 1)
        load_weights("y", 0)
        place_scales(1)
        nc.sync.dma_start(cen_t[:], cen)
        load_weights("y", 1)
        load_weights("b", 0)
        load_weights("b", 1)
        nc.sync.dma_start(pos_t["a"][:], pos1)
        nc.sync.dma_start(pos_t["b"][:], pos2)

        by_block = [(mb, h) for mb in range(BLOCKS) for h in range(HALVES)]
        by_bank = [(mb, h, o) for mb, h in by_block for o in range(PASSES)]
        gather_words(0)
        stage("a", 0, BLOCKS)
        interleave(on_scalar, "a", 0)
        quantize("a", 0, BLOCKS)
        for mb, h in by_block:
            multiply("a", 0, 0, mb, h)
        gather_words(1)
        stage("a", BLOCKS, BLOCKS)
        for mb in range(BLOCKS):
            interleave(on_scalar, "a", 1, mb, 1)
            quantize("a", BLOCKS + mb, 1)
            for h in range(HALVES):
                multiply("a", 1, 0, mb, h)

        def last_pass(name, first_bank):
            for mb in range(BLOCKS):
                interleave(nc.vector.tensor_copy, name, 1, mb, 1)
            quantize(name, 0, 3)
            quantize(name, 3, 1)
            for mb, h, o in by_bank:
                multiply(name, o, first_bank, mb, h)

        stage("y", 0, 3)
        stage("y", 3, 1)
        interleave(nc.vector.tensor_copy, "y", 0)
        last_pass("y", 4)
        for mb, h in by_block:
            evacuate(tanh, "a", mb, h)
        stage("b", 0, 3)
        stage("b", 3, 1)
        interleave(nc.vector.tensor_copy, "b", 0)
        last_pass("b", 0)
        for mb, h in by_block[:-1]:
            evacuate(nc.vector.tensor_copy, "y", mb, h, ["raw_b1", "rounded_b0"][mb])
        for mb in range(BLOCKS):
            gate("a", mb, "mask")
        evacuate(on_scalar, "y", 1, 1)
        for h in range(HALVES):
            evacuate(tanh, "b", 0, h)
        pieces = [(0, 256), (256, 256)]
        for first, width in pieces:
            gate("b", 0, "sample", first, width)
        for h in range(HALVES):
            evacuate(tanh, "b", 1, h)
        for first, width in pieces:
            gate("b", 1, "sample", first, width)
        term("a", 0, "sample")
        term("a", 1, "sample")
        for first, width in pieces:
            term("b", 0, "mask", first, width)
        for first, width in pieces:
            finish(0, first, width)
        store(0)
        for first, width in pieces:
            term("b", 1, "mask", first, width)
        for first, width in pieces:
            finish(1, first, width)
            store(1, first, width)
